import numpy as np
import ml_dtypes


def mxq(x, axis, fmt="e4m3"):
    dtype, down = {"e4m3": (ml_dtypes.float8_e4m3fn, 7), "e5m2": (ml_dtypes.float8_e5m2, 14)}[fmt]
    v = np.moveaxis(np.asarray(x, np.float32).astype(ml_dtypes.bfloat16).astype(np.float64), axis, -1)
    blocks = v.reshape(v.shape[:-1] + (-1, 32))
    amax = np.abs(blocks).max(-1, keepdims=True)
    byte = np.maximum(np.where(amax > 0, np.frexp(amax)[1] - 1 + 127, 0) - down, 1)
    scale = np.exp2(byte - 127.0)
    codes = (blocks / scale).astype(np.float32).astype(dtype).astype(np.float64)
    return np.moveaxis((codes * scale).reshape(v.shape), -1, axis)


WIDE = False


def mx_kscale(k):
    if not WIDE:
        return np.ones(k)
    levels = np.array([30, -30])
    if k % 512:
        return np.exp2(np.random.permutation(np.resize(levels, k // 32))).repeat(32)
    a = np.empty((k // 512, 16))
    for p in range(k // 512):
        a[p, :8] = np.random.permutation(np.resize(levels, 8))
        for g in range(8):
            far = levels[np.abs(levels - a[p, g]) >= 10]
            a[p, g + 8] = far[np.random.randint(len(far))]
    return np.exp2(a.ravel()).repeat(32)


def f64(x):
    return np.asarray(x).astype(np.float64)


def striped(idx):
    return np.tile(idx.reshape(-1, 16).T, (8, 1)).astype(np.uint16)


def unstriped(offs):
    return offs[:16].T.reshape(-1).astype(np.int64)


def bf(x):
    return np.asarray(x, np.float32).astype(ml_dtypes.bfloat16)


E2M1 = np.array([0.0, 0.5, 1.0, 1.5, 2.0, 3.0, 4.0, 6.0, -0.0, -0.5, -1.0, -1.5, -2.0, -3.0, -4.0, -6.0])


def pack_weight(w, fmt):
    k, n = w.shape
    w = f64(bf(w)).reshape(k // 32, 32, n)
    amax = np.abs(w).max(1)
    if fmt in ("e4m3", "e5m2"):
        byte = np.frexp(amax)[1] - 1 + 127 - (7 if fmt == "e4m3" else 14)
    else:
        mant, ex = np.frexp(amax / 6.0)
        byte = np.where(mant > 0.5, ex, ex - 1) + 127
    byte = np.clip(np.where(amax > 0, byte, 1), 1, 254)
    scaled = (w * np.exp2(127.0 - byte)[:, None, :]).reshape(k, n).astype(np.float32)
    by_word = np.ascontiguousarray(scaled.reshape(k // 512, 128, 4, n).transpose(0, 1, 3, 2))
    if fmt in ("e4m3", "e5m2"):
        words = by_word.astype(ml_dtypes.float8_e4m3fn if fmt == "e4m3" else ml_dtypes.float8_e5m2).view(np.uint8)
    else:
        c = by_word.astype(ml_dtypes.float4_e2m1fn).view(np.uint8) & 0xF
        words = c[..., 0::2] | (c[..., 1::2] << 4)
    return np.ascontiguousarray(words), np.ascontiguousarray(byte.astype(np.uint8).reshape(k // 512, 16, n))


def unpack_weight(words, scales, fmt):
    g, p, n, _ = words.shape
    if fmt in ("e4m3", "e5m2"):
        vals = np.ascontiguousarray(words).view(ml_dtypes.float8_e4m3fn if fmt == "e4m3" else ml_dtypes.float8_e5m2).astype(np.float64)
    else:
        nib = np.empty((g, p, n, 4), np.uint8)
        nib[..., 0::2] = words & 0xF
        nib[..., 1::2] = words >> 4
        vals = E2M1[nib]
    vals = vals * np.repeat(np.exp2(scales.astype(np.float64) - 127.0), 8, axis=1)[..., None]
    return vals.transpose(0, 1, 3, 2).reshape(g * 512, n)


K, T, S, H, N = 1024, 2048, 1024, 1024, 512

def setup_inputs():
    n = np.random.standard_normal
    s = mx_kscale(K)[:, None]
    u = mx_kscale(H)[:, None]
    tab_words, tab_scales = pack_weight(n((K, T)) * np.exp(1.0 * n((1, T))) * s, "e5m2")
    wd_words, wd_scales = pack_weight(0.4 * n((K, N)) / np.sqrt(K) / s, "e4m3")
    return {
        "tab_words": tab_words,
        "tab_scales": tab_scales,
        "offs": striped(np.random.permutation(T)[:S]),
        "w1": (0.6 * n((K, H)) / np.sqrt(K) / s).astype(np.float32),
        "g": (np.exp(0.3 * n(H)) * u[:, 0]).astype(np.float32),
        "w2": (2.0 * n((H, N)) / np.sqrt(H) / u).astype(np.float32),
        "wd_words": wd_words,
        "wd_scales": wd_scales,
    }

def reference(tab_words, tab_scales, offs, w1, g, w2, wd_words, wd_scales):
    v = unpack_weight(tab_words, tab_scales, "e5m2")[:, unstriped(offs)]
    wd = unpack_weight(wd_words, wd_scales, "e4m3")
    a = mxq(f64(w1), 0, "e4m3").T @ v
    h = f64(g)[:, None] * np.tanh(a)
    y = mxq(f64(w2), 0, "e4m3").T @ mxq(h, 0, "e4m3")
    d = wd.T @ v
    return y * (1.0 / (1.0 + np.exp(-d)))

@@ -1,0 +1,217 @@
+from contextlib import ExitStack
+
+import concourse.mybir as mybir
+
+K, T, S, H, N = 1024, 2048, 1024, 1024, 512
+FLOPS = 2 * S * (K * H + H * N + K * N)
+
+F32 = mybir.dt.float32
+BF16 = mybir.dt.bfloat16
+I32 = mybir.dt.int32
+U32 = mybir.dt.uint32
+U16 = mybir.dt.uint16
+U8 = mybir.dt.uint8
+E4M3 = mybir.dt.float8_e4m3fn_x4
+E5M2 = mybir.dt.float8_e5m2_x4
+ACT = mybir.ActivationFunctionType
+MULT = mybir.AluOpType.mult
+
+P = 128
+PACK = 4
+PASS = P * PACK
+HALF = 512
+
+
+def tile_list_aligned_error_gate_kernel(tc, tab_words, tab_scales, offs, w1, g, w2, wd_words, wd_scales, out):
+    nc = tc.nc
+    with ExitStack() as ctx:
+        keep = ctx.enter_context(tc.tile_pool(name="keep", bufs=1))
+        ring = ctx.enter_context(tc.tile_pool(name="ring", bufs=3))
+        stage = ctx.enter_context(tc.tile_pool(name="stage", bufs=4))
+        psum = ctx.enter_context(tc.psum_pool(name="psum", bufs=4))
+
+        offsets = keep.tile([P, S // 16], U16, name="offsets")
+        warm_in = stage.tile([P, 1], F32, name="warm_in", tag="stage", align_bytes=64)
+        warm_out = stage.tile([P, 1], F32, name="warm_out", tag="stage", align_bytes=64)
+        table = [stage.tile([P, T], I32, name=f"table{a}", tag="stage", align_bytes=64) for a in range(2)]
+        table_sc = stage.tile([P, T // 4], I32, name="table_sc", tag="stage", align_bytes=64)
+        v_codes = [keep.tile([P, S], U32, name=f"v_codes{a}", align_bytes=64) for a in range(2)]
+        picked_sc = keep.tile([P, S], U8, name="picked_sc", align_bytes=64)
+        moved_sc = keep.tile([P, S // 4], I32, name="moved_sc", align_bytes=64)
+        v_sc = [picked_sc[:], moved_sc[:].bitcast(U8)]
+        wd_codes = stage.tile([P, 2, N], I32, name="wd_codes", tag="stage", align_bytes=64)
+        wd_sc = keep.tile([P, 2, N // 4], I32, name="wd_sc", align_bytes=64)
+        gain = keep.tile([P, 2, PACK], F32, name="gain")
+        w1_raw = {(a, b): stage.tile([P, PACK, PASS], F32, name=f"w1_raw{a}{b}", tag="stage", align_bytes=64) for b in range(2) for a in range(2)}
+        w2_raw = [stage.tile([P, PACK, N], F32, name=f"w2_raw{b}", tag="stage", align_bytes=64) for b in range(2)]
+        w1_bf = {(a, b): keep.tile([P, PACK, P, PACK], BF16, name=f"w1_bf{a}{b}", align_bytes=64) for a in range(2) for b in range(2)}
+        w2_bf = [keep.tile([P, N, PACK], BF16, name=f"w2_bf{b}", align_bytes=64) for b in range(2)]
+        w1_codes = {(a, b): keep.tile([P, PASS], U32, name=f"w1_codes{a}{b}", align_bytes=64) for a in range(2) for b in range(2)}
+        w1_sc = {(a, b): keep.tile([P, PASS], U8, name=f"w1_sc{a}{b}", align_bytes=64) for a in range(2) for b in range(2)}
+        w2_codes = [keep.tile([P, N], U32, name=f"w2_codes{b}", align_bytes=64) for b in range(2)]
+        w2_sc = [keep.tile([P, N], U8, name=f"w2_sc{b}", align_bytes=64) for b in range(2)]
+        h_codes = [keep.tile([P, S], U32, name=f"h_codes{b}", align_bytes=64) for b in range(2)]
+        h_sc = [keep.tile([P, S], U8, name=f"h_sc{b}", align_bytes=64) for b in range(2)]
+        gate = keep.tile([P, N // P, S], F32, name="gate")
+        bounded = {}
+        h_bf = {}
+
+        def load_table_scales():
+            for q in range(4):
+                nc.sync.dma_start(out=table_sc[32 * q : 32 * q + 4, :], in_=tab_scales[0, 4 * q : 4 * q + 4, :].bitcast(I32))
+            nc.sync.dma_start(out=table_sc[8:24, :], in_=tab_scales[1].bitcast(I32))
+
+        def load_table(a):
+            nc.sync.dma_start(out=table[a][:], in_=tab_words[a].rearrange("p t i -> p (t i)").bitcast(I32))
+
+        def load_w1(a, b, c0, c1):
+            rows = w1[PASS * a : PASS * (a + 1), PASS * b + c0 : PASS * b + c1]
+            nc.sync.dma_start(out=w1_raw[a, b][:, :, c0:c1], in_=rows.rearrange("(p j) c -> p j c", j=PACK))
+
+        def load_w2(b):
+            nc.sync.dma_start(out=w2_raw[b][:], in_=w2[PASS * b : PASS * (b + 1), :].rearrange("(p j) c -> p j c", j=PACK))
+
+        def gather_scales():
+            nc.vector.tensor_copy(picked_sc[:], table_sc[:].bitcast(U8).indirect(offsets[:]))
+            for q in range(4):
+                nc.sync.dma_start(out=moved_sc[32 * q : 32 * q + 4, :], in_=picked_sc[8 + 4 * q : 12 + 4 * q, :].bitcast(I32))
+
+        def gather_codes(a, s):
+            window = table[a][:].bitcast(U32).indirect(offsets[:, 32 * s : 32 * (s + 1)])
+            nc.vector.tensor_copy(v_codes[a][:, HALF * s : HALF * (s + 1)], window)
+
+        def cast(engine, dst, src):
+            if engine == "vector":
+                nc.vector.tensor_copy(out=dst, in_=src)
+            else:
+                nc.scalar.activation(out=dst, in_=src, func=ACT.Copy)
+
+        def cast_w1(engine, a, b, m0, m1):
+            dst = w1_bf[a, b][:, :, m0:m1, :].rearrange("p t m j -> p m j t")
+            src = w1_raw[a, b][:, :, PACK * m0 : PACK * m1].rearrange("p j (m t) -> p m j t", t=PACK)
+            cast(engine, dst, src)
+
+        def cast_w2(engine, b, c0, c1):
+            dst = w2_bf[b][:, c0:c1, :].rearrange("p (c i) j -> p c j i", i=4)
+            src = w2_raw[b][:, :, c0:c1].rearrange("p j (c i) -> p c j i", i=4)
+            cast(engine, dst, src)
+
+        def quantize_w1(a, b):
+            nc.vector.quantize_mx(out=w1_codes[a, b][:].bitcast(E4M3), scales=w1_sc[a, b][:], in_=w1_bf[a, b][:].rearrange("p t m j -> p (t m j)"))
+
+        def quantize_w2(b):
+            nc.vector.quantize_mx(out=w2_codes[b][:].bitcast(E4M3), scales=w2_sc[b][:], in_=w2_bf[b][:].rearrange("p c j -> p (c j)"))
+
+        def table_product(codes, scales, s):
+            cols = slice(HALF * s, HALF * (s + 1))
+            acc = psum.tile([P, HALF], F32, name="acc")
+            for a in range(2):
+                nc.tensor.matmul_mx(out=acc[:], lhsT=codes[a].bitcast(E4M3), lhsT_scale=scales[a],
+                                    rhs=v_codes[a][:, cols].bitcast(E5M2), rhs_scale=v_sc[a][:, cols],
+                                    start=(a == 0), stop=(a == 1))
+            return acc
+
+        def bound(b, s):
+            bounded[b, s] = ring.tile([P, PACK, HALF], F32, name="bounded")
+            for t in range(PACK):
+                cols = slice(P * t, P * (t + 1))
+                acc = table_product([w1_codes[a, b][:, cols] for a in range(2)], [w1_sc[a, b][:, cols] for a in range(2)], s)
+                nc.scalar.activation(out=bounded[b, s][:, t, :], in_=acc[:], func=ACT.Tanh)
+
+        def gate_half(s):
+            for n in range(N // P):
+                cols = slice(P * n, P * (n + 1))
+                acc = table_product([wd_codes[:, a, cols] for a in range(2)], [wd_sc[:, a, :].bitcast(U8)[:, cols] for a in range(2)], s)
+                nc.scalar.activation(out=gate[:, n, HALF * s : HALF * (s + 1)], in_=acc[:], func=ACT.Sigmoid)
+
+        def apply_gain(b, s, c0, c1):
+            if (b, s) not in h_bf:
+                h_bf[b, s] = ring.tile([P, HALF, PACK], BF16, name="h_bf", align_bytes=64)
+            nc.vector.tensor_tensor(
+                out=h_bf[b, s][:, c0:c1, :].rearrange("p (c i) t -> p c t i", i=4),
+                in0=bounded[b, s][:, :, c0:c1].rearrange("p t (c i) -> p c t i", i=4),
+                in1=gain[:, b, :].unsqueeze(1).unsqueeze(3).to_broadcast([P, (c1 - c0) // 4, PACK, 4]),
+                op=MULT,
+            )
+
+        def quantize_h(b, s, c0, c1):
+            cols = slice(HALF * s + c0, HALF * s + c1)
+            nc.vector.quantize_mx(out=h_codes[b][:, cols].bitcast(E4M3), scales=h_sc[b][:, cols], in_=h_bf[b, s][:, c0:c1, :].rearrange("p c t -> p (c t)"))
+
+        def finish(c0, c1):
+            cols = slice(c0, c1)
+            tiles = HALF // (c1 - c0)
+            for n0 in range(0, N // P, tiles):
+                y = psum.tile([P, tiles, c1 - c0], F32, name="y")
+                for i in range(tiles):
+                    rows = slice(P * (n0 + i), P * (n0 + i + 1))
+                    for b in range(2):
+                        nc.tensor.matmul_mx(out=y[:, i, :], lhsT=w2_codes[b][:, rows].bitcast(E4M3), lhsT_scale=w2_sc[b][:, rows],
+                                            rhs=h_codes[b][:, cols].bitcast(E4M3), rhs_scale=h_sc[b][:, cols],
+                                            start=(b == 0), stop=(b == 1))
+                result = ring.tile([P, tiles, c1 - c0], F32, name="result", bufs=4)
+                nc.vector.tensor_tensor(out=result[:], in0=y[:], in1=gate[:, n0 : n0 + tiles, cols], op=MULT)
+                nc.sync.dma_start(out=out[P * n0 : P * (n0 + tiles), cols].rearrange("(i p) s -> p i s", p=P), in_=result[:])
+
+        nc.sync.dma_start(offsets[:], offs)
+        load_table(0)
+        nc.vector.memset(table_sc[:], 0)
+        nc.gpsimd.memset(warm_in[:], 0.0)
+        nc.gpsimd.memset(wd_sc[:], 0)
+        nc.gpsimd.memset(moved_sc[:], 0)
+        nc.scalar.dma_start(out=gain[:], in_=g.rearrange("(b p t) -> p b t", b=2, t=PACK))
+        load_table_scales()
+        nc.scalar.activation(out=warm_out[:], in_=warm_in[:], func=ACT.Sigmoid)
+        load_w1(0, 0, 0, PASS // 2)
+        load_w1(0, 0, PASS // 2, PASS)
+        load_table(1)
+        for q in range(4):
+            nc.gpsimd.dma_start(out=wd_sc[32 * q : 32 * q + 4, :, :], in_=wd_scales[:, 4 * q : 4 * q + 4, :].rearrange("a r c -> r a c").bitcast(I32))
+
+        gather_scales()
+        load_w1(1, 0, 0, PASS // 2)
+        load_w1(1, 0, PASS // 2, PASS)
+        gather_codes(0, 0)
+        cast_w1("scalar", 0, 0, 0, P // 2)
+        cast_w1("scalar", 0, 0, P // 2, P)
+        gather_codes(0, 1)
+        load_w1(0, 1, 0, PASS)
+        load_w1(1, 1, 0, PASS)
+        gather_codes(1, 0)
+        quantize_w1(0, 0)
+        cast_w1("scalar", 1, 0, 0, P // 2)
+        cast_w1("scalar", 1, 0, P // 2, 3 * P // 4 - 8)
+        cast_w1("vector", 1, 0, 3 * P // 4 - 8, P)
+        nc.sync.dma_start(out=wd_codes[:], in_=wd_words.rearrange("a p c i -> p a (c i)").bitcast(I32))
+        quantize_w1(1, 0)
+        gather_codes(1, 1)
+        load_w2(0)
+        bound(0, 0)
+        cast_w1("vector", 0, 1, 0, P)
+        load_w2(1)
+        cast_w1("scalar", 1, 1, 0, P)
+        quantize_w1(0, 1)
+        apply_gain(0, 0, 0, HALF)
+        bound(0, 1)
+        quantize_w1(1, 1)
+        quantize_h(0, 0, 0, HALF)
+        cast_w2("vector", 0, 0, N // 2)
+        bound(1, 0)
+        apply_gain(0, 1, 0, HALF)
+        cast_w2("scalar", 0, N // 2, N)
+        cast_w2("scalar", 1, 0, N)
+        quantize_h(0, 1, 0, HALF)
+        apply_gain(1, 0, 0, HALF)
+        bound(1, 1)
+        quantize_w2(0)
+        quantize_h(1, 0, 0, HALF)
+        quantize_w2(1)
+        gate_half(0)
+        apply_gain(1, 1, 0, HALF // 2)
+        apply_gain(1, 1, HALF // 2, HALF)
+        quantize_h(1, 1, 0, HALF // 2)
+        finish(0, HALF)
+        quantize_h(1, 1, HALF // 2, HALF)
+        gate_half(1)
+        finish(HALF, HALF + HALF // 2)
+        finish(HALF + HALF // 2, S)

@@ -15,35 +15,41 @@ E4M3 = mybir.dt.float8_e4m3fn_x4
 E5M2 = mybir.dt.float8_e5m2_x4
 ACT = mybir.ActivationFunctionType
 MULT = mybir.AluOpType.mult
+ADD = mybir.AluOpType.add
 
 P = 128
 PACK = 4
 PASS = P * PACK
 HALF = 512
+PIECE = 256
+SLOT = 4096
 
 
 def tile_list_aligned_error_gate_kernel(tc, tab_words, tab_scales, offs, w1, g, w2, wd_words, wd_scales, out):
     nc = tc.nc
     with ExitStack() as ctx:
         keep = ctx.enter_context(tc.tile_pool(name="keep", bufs=1))
-        ring = ctx.enter_context(tc.tile_pool(name="ring", bufs=3))
-        stage = ctx.enter_context(tc.tile_pool(name="stage", bufs=4))
-        psum = ctx.enter_context(tc.psum_pool(name="psum", bufs=4))
+        stage = ctx.enter_context(tc.tile_pool(name="stage", bufs=1))
+        psum = ctx.enter_context(tc.psum_pool(name="psum", bufs=1))
 
         offsets = keep.tile([P, S // 16], U16, name="offsets")
-        warm_in = stage.tile([P, 1], F32, name="warm_in", tag="stage", align_bytes=64)
-        warm_out = stage.tile([P, 1], F32, name="warm_out", tag="stage", align_bytes=64)
-        table = [stage.tile([P, T], I32, name=f"table{a}", tag="stage", align_bytes=64) for a in range(2)]
-        table_sc = stage.tile([P, T // 4], I32, name="table_sc", tag="stage", align_bytes=64)
+        warm_in = stage.tile([P, 16], F32, name="warm_in", offset=4 * SLOT - 32)
+        warm_out = stage.tile([P, 16], F32, name="warm_out", offset=6 * SLOT - 32)
+        table = [stage.tile([P, T], I32, name=f"table{a}", offset=(2 * SLOT, 6 * SLOT)[a], align_bytes=64) for a in range(2)]
+        table_sc = stage.tile([P, T // 4], I32, name="table_sc", offset=8 * SLOT, align_bytes=64)
+        gain = stage.tile([P, 2, PACK], F32, name="gain", offset=8 * SLOT)
+        late = 8 * SLOT + 64
+        w1_at = {(0, 0, 0): 0, (0, 0, 1): SLOT, (1, 0, 0): 4 * SLOT, (1, 0, 1): 5 * SLOT,
+                 (0, 1, 0): late, (0, 1, 1): 4 * SLOT, (1, 1, 0): 5 * SLOT, (1, 1, 1): 2 * SLOT}
+        w2_at = {(0, 0): 3 * SLOT, (0, 1): 6 * SLOT, (1, 0): late, (1, 1): 4 * SLOT}
+        w1_raw = {k: stage.tile([P, PACK, PIECE], F32, name="w1_raw%d%d%d" % k, offset=v) for k, v in w1_at.items()}
+        w2_raw = {k: stage.tile([P, PACK, PIECE], F32, name="w2_raw%d%d" % k, offset=v) for k, v in w2_at.items()}
+        wd_codes = stage.tile([P, 2, N], I32, name="wd_codes", offset=7 * SLOT, align_bytes=64)
         v_codes = [keep.tile([P, S], U32, name=f"v_codes{a}", align_bytes=64) for a in range(2)]
         picked_sc = keep.tile([P, S], U8, name="picked_sc", align_bytes=64)
         moved_sc = keep.tile([P, S // 4], I32, name="moved_sc", align_bytes=64)
         v_sc = [picked_sc[:], moved_sc[:].bitcast(U8)]
-        wd_codes = stage.tile([P, 2, N], I32, name="wd_codes", tag="stage", align_bytes=64)
         wd_sc = keep.tile([P, 2, N // 4], I32, name="wd_sc", align_bytes=64)
-        gain = keep.tile([P, 2, PACK], F32, name="gain")
-        w1_raw = {(a, b): stage.tile([P, PACK, PASS], F32, name=f"w1_raw{a}{b}", tag="stage", align_bytes=64) for b in range(2) for a in range(2)}
-        w2_raw = [stage.tile([P, PACK, N], F32, name=f"w2_raw{b}", tag="stage", align_bytes=64) for b in range(2)]
         w1_bf = {(a, b): keep.tile([P, PACK, P, PACK], BF16, name=f"w1_bf{a}{b}", align_bytes=64) for a in range(2) for b in range(2)}
         w2_bf = [keep.tile([P, N, PACK], BF16, name=f"w2_bf{b}", align_bytes=64) for b in range(2)]
         w1_codes = {(a, b): keep.tile([P, PASS], U32, name=f"w1_codes{a}{b}", align_bytes=64) for a in range(2) for b in range(2)}
@@ -53,8 +59,16 @@ def tile_list_aligned_error_gate_kernel(tc, tab_words, tab_scales, offs, w1, g, 
         h_codes = [keep.tile([P, S], U32, name=f"h_codes{b}", align_bytes=64) for b in range(2)]
         h_sc = [keep.tile([P, S], U8, name=f"h_sc{b}", align_bytes=64) for b in range(2)]
         gate = keep.tile([P, N // P, S], F32, name="gate")
-        bounded = {}
-        h_bf = {}
+        bounded = {(b, s): keep.tile([P, PACK, HALF], F32, name=f"bounded{b}{s}") for b in range(2) for s in range(2)}
+        h_bf = {(b, s): keep.tile([P, HALF, PACK], BF16, name=f"h_bf{b}{s}", align_bytes=64) for b in range(2) for s in range(2)}
+        banks = [psum.tile([P, HALF], F32, name=f"bank{i}") for i in range(8)]
+        results = [keep.tile([P, HALF], F32, name=f"result{i}") for i in range(8)]
+        used_banks = []
+        used_results = []
+
+        def next_bank():
+            used_banks.append(len(used_banks) % len(banks))
+            return banks[used_banks[-1]]
 
         def load_table_scales():
             for q in range(4):
@@ -66,10 +80,17 @@ def tile_list_aligned_error_gate_kernel(tc, tab_words, tab_scales, offs, w1, g, 
 
         def load_w1(a, b, c0, c1):
             rows = w1[PASS * a : PASS * (a + 1), PASS * b + c0 : PASS * b + c1]
-            nc.sync.dma_start(out=w1_raw[a, b][:, :, c0:c1], in_=rows.rearrange("(p j) c -> p j c", j=PACK))
+            nc.sync.dma_start(out=w1_raw[a, b, c0 // PIECE][:], in_=rows.rearrange("(p j) c -> p j c", j=PACK))
 
-        def load_w2(b):
-            nc.sync.dma_start(out=w2_raw[b][:], in_=w2[PASS * b : PASS * (b + 1), :].rearrange("(p j) c -> p j c", j=PACK))
+        def load_w2(b, c0, c1):
+            rows = w2[PASS * b : PASS * (b + 1), c0:c1]
+            nc.sync.dma_start(out=w2_raw[b, c0 // PIECE][:], in_=rows.rearrange("(p j) c -> p j c", j=PACK))
+
+        def load_wd():
+            nc.sync.dma_start(out=wd_codes[:], in_=wd_words.rearrange("a p c i -> p a (c i)").bitcast(I32))
+
+        def load_gain():
+            nc.sync.dma_start(out=gain[:], in_=g.rearrange("(b p t) -> p b t", b=2, t=PACK))
 
         def gather_scales():
             nc.vector.tensor_copy(picked_sc[:], table_sc[:].bitcast(U8).indirect(offsets[:]))
@@ -83,17 +104,21 @@ def tile_list_aligned_error_gate_kernel(tc, tab_words, tab_scales, offs, w1, g, 
         def cast(engine, dst, src):
             if engine == "vector":
                 nc.vector.tensor_copy(out=dst, in_=src)
+            elif engine == "gpsimd":
+                nc.gpsimd.tensor_scalar(out=dst, in0=src, scalar1=1.0, scalar2=0.0, op0=MULT, op1=ADD)
             else:
                 nc.scalar.activation(out=dst, in_=src, func=ACT.Copy)
 
         def cast_w1(engine, a, b, m0, m1):
+            piece, c0 = divmod(PACK * m0, PIECE)
             dst = w1_bf[a, b][:, :, m0:m1, :].rearrange("p t m j -> p m j t")
-            src = w1_raw[a, b][:, :, PACK * m0 : PACK * m1].rearrange("p j (m t) -> p m j t", t=PACK)
+            src = w1_raw[a, b, piece][:, :, c0 : c0 + PACK * (m1 - m0)].rearrange("p j (m t) -> p m j t", t=PACK)
             cast(engine, dst, src)
 
         def cast_w2(engine, b, c0, c1):
+            piece, first = divmod(c0, PIECE)
             dst = w2_bf[b][:, c0:c1, :].rearrange("p (c i) j -> p c j i", i=4)
-            src = w2_raw[b][:, :, c0:c1].rearrange("p j (c i) -> p c j i", i=4)
+            src = w2_raw[b, piece][:, :, first : first + c1 - c0].rearrange("p j (c i) -> p c j i", i=4)
             cast(engine, dst, src)
 
         def quantize_w1(a, b):
@@ -104,33 +129,31 @@ def tile_list_aligned_error_gate_kernel(tc, tab_words, tab_scales, offs, w1, g, 
 
         def table_product(codes, scales, s):
             cols = slice(HALF * s, HALF * (s + 1))
-            acc = psum.tile([P, HALF], F32, name="acc")
+            acc = next_bank()
             for a in range(2):
                 nc.tensor.matmul_mx(out=acc[:], lhsT=codes[a].bitcast(E4M3), lhsT_scale=scales[a],
                                     rhs=v_codes[a][:, cols].bitcast(E5M2), rhs_scale=v_sc[a][:, cols],
                                     start=(a == 0), stop=(a == 1))
             return acc
 
-        def bound(b, s):
-            bounded[b, s] = ring.tile([P, PACK, HALF], F32, name="bounded")
-            for t in range(PACK):
+        def bound(b, s, slots):
+            for t in slots:
                 cols = slice(P * t, P * (t + 1))
                 acc = table_product([w1_codes[a, b][:, cols] for a in range(2)], [w1_sc[a, b][:, cols] for a in range(2)], s)
                 nc.scalar.activation(out=bounded[b, s][:, t, :], in_=acc[:], func=ACT.Tanh)
 
-        def gate_half(s):
-            for n in range(N // P):
+        def gate_half(s, tiles):
+            for n in tiles:
                 cols = slice(P * n, P * (n + 1))
                 acc = table_product([wd_codes[:, a, cols] for a in range(2)], [wd_sc[:, a, :].bitcast(U8)[:, cols] for a in range(2)], s)
                 nc.scalar.activation(out=gate[:, n, HALF * s : HALF * (s + 1)], in_=acc[:], func=ACT.Sigmoid)
 
-        def apply_gain(b, s, c0, c1):
-            if (b, s) not in h_bf:
-                h_bf[b, s] = ring.tile([P, HALF, PACK], BF16, name="h_bf", align_bytes=64)
-            nc.vector.tensor_tensor(
+        def apply_gain(b, s, c0, c1, engine):
+            factors = gain[:, b, :]
+            (nc.vector if engine == "vector" else nc.gpsimd).tensor_tensor(
                 out=h_bf[b, s][:, c0:c1, :].rearrange("p (c i) t -> p c t i", i=4),
                 in0=bounded[b, s][:, :, c0:c1].rearrange("p t (c i) -> p c t i", i=4),
-                in1=gain[:, b, :].unsqueeze(1).unsqueeze(3).to_broadcast([P, (c1 - c0) // 4, PACK, 4]),
+                in1=factors.unsqueeze(1).unsqueeze(3).to_broadcast([P, (c1 - c0) // 4, PACK, 4]),
                 op=MULT,
             )
 
@@ -138,80 +161,92 @@ def tile_list_aligned_error_gate_kernel(tc, tab_words, tab_scales, offs, w1, g, 
             cols = slice(HALF * s + c0, HALF * s + c1)
             nc.vector.quantize_mx(out=h_codes[b][:, cols].bitcast(E4M3), scales=h_sc[b][:, cols], in_=h_bf[b, s][:, c0:c1, :].rearrange("p c t -> p (c t)"))
 
-        def finish(c0, c1):
+        def finish(c0, c1, firsts):
             cols = slice(c0, c1)
             tiles = HALF // (c1 - c0)
-            for n0 in range(0, N // P, tiles):
-                y = psum.tile([P, tiles, c1 - c0], F32, name="y")
+            for n0 in firsts:
+                y = next_bank()[:].rearrange("p (i s) -> p i s", i=tiles)
                 for i in range(tiles):
                     rows = slice(P * (n0 + i), P * (n0 + i + 1))
                     for b in range(2):
                         nc.tensor.matmul_mx(out=y[:, i, :], lhsT=w2_codes[b][:, rows].bitcast(E4M3), lhsT_scale=w2_sc[b][:, rows],
                                             rhs=h_codes[b][:, cols].bitcast(E4M3), rhs_scale=h_sc[b][:, cols],
                                             start=(b == 0), stop=(b == 1))
-                result = ring.tile([P, tiles, c1 - c0], F32, name="result", bufs=4)
-                nc.vector.tensor_tensor(out=result[:], in0=y[:], in1=gate[:, n0 : n0 + tiles, cols], op=MULT)
-                nc.sync.dma_start(out=out[P * n0 : P * (n0 + tiles), cols].rearrange("(i p) s -> p i s", p=P), in_=result[:])
+                used_results.append(n0)
+                result = results[len(used_results) - 1][:].rearrange("p (i s) -> p i s", i=tiles)
+                nc.vector.tensor_tensor(out=result, in0=y, in1=gate[:, n0 : n0 + tiles, cols], op=MULT)
+                nc.sync.dma_start(out=out[P * n0 : P * (n0 + tiles), cols].rearrange("(i p) s -> p i s", p=P), in_=result)
 
         nc.sync.dma_start(offsets[:], offs)
-        load_table(0)
         nc.vector.memset(table_sc[:], 0)
         nc.gpsimd.memset(warm_in[:], 0.0)
         nc.gpsimd.memset(wd_sc[:], 0)
         nc.gpsimd.memset(moved_sc[:], 0)
-        nc.scalar.dma_start(out=gain[:], in_=g.rearrange("(b p t) -> p b t", b=2, t=PACK))
         load_table_scales()
         nc.scalar.activation(out=warm_out[:], in_=warm_in[:], func=ACT.Sigmoid)
-        load_w1(0, 0, 0, PASS // 2)
-        load_w1(0, 0, PASS // 2, PASS)
-        load_table(1)
         for q in range(4):
             nc.gpsimd.dma_start(out=wd_sc[32 * q : 32 * q + 4, :, :], in_=wd_scales[:, 4 * q : 4 * q + 4, :].rearrange("a r c -> r a c").bitcast(I32))
-
+        load_w1(0, 0, 0, 256)
+        load_w1(0, 0, 256, 512)
+        load_table(0)
+        load_w1(1, 0, 0, 256)
+        load_w1(1, 0, 256, 512)
+        load_table(1)
+        cast_w1("vector", 0, 0, 0, 64)
+        cast_w1("scalar", 0, 0, 64, 128)
         gather_scales()
-        load_w1(1, 0, 0, PASS // 2)
-        load_w1(1, 0, PASS // 2, PASS)
+        load_w1(0, 1, 0, 256)
+        load_gain()
         gather_codes(0, 0)
-        cast_w1("scalar", 0, 0, 0, P // 2)
-        cast_w1("scalar", 0, 0, P // 2, P)
+        cast_w1("scalar", 1, 0, 0, 64)
+        load_w1(0, 1, 256, 512)
         gather_codes(0, 1)
-        load_w1(0, 1, 0, PASS)
-        load_w1(1, 1, 0, PASS)
-        gather_codes(1, 0)
+        load_w1(1, 1, 256, 512)
+        load_w2(0, 0, 256)
+        cast_w1("scalar", 1, 0, 64, 128)
+        load_w1(1, 1, 0, 256)
         quantize_w1(0, 0)
-        cast_w1("scalar", 1, 0, 0, P // 2)
-        cast_w1("scalar", 1, 0, P // 2, 3 * P // 4 - 8)
-        cast_w1("vector", 1, 0, 3 * P // 4 - 8, P)
-        nc.sync.dma_start(out=wd_codes[:], in_=wd_words.rearrange("a p c i -> p a (c i)").bitcast(I32))
         quantize_w1(1, 0)
+        gather_codes(1, 0)
+        cast_w1("scalar", 0, 1, 0, 64)
+        load_w2(1, 0, 256)
         gather_codes(1, 1)
-        load_w2(0)
-        bound(0, 0)
-        cast_w1("vector", 0, 1, 0, P)
-        load_w2(1)
-        cast_w1("scalar", 1, 1, 0, P)
+        load_w2(0, 256, 512)
+        load_wd()
+        bound(0, 0, [0, 1, 2, 3])
+        cast_w1("vector", 0, 1, 64, 128)
+        load_w2(1, 256, 512)
+        cast_w1("vector", 1, 1, 64, 128)
         quantize_w1(0, 1)
-        apply_gain(0, 0, 0, HALF)
-        bound(0, 1)
+        cast_w1("scalar", 1, 1, 0, 64)
+        cast_w2("vector", 0, 0, 256)
+        apply_gain(0, 0, 0, 512, "vector")
+        bound(0, 1, [0, 1, 2, 3])
         quantize_w1(1, 1)
-        quantize_h(0, 0, 0, HALF)
-        cast_w2("vector", 0, 0, N // 2)
-        bound(1, 0)
-        apply_gain(0, 1, 0, HALF)
-        cast_w2("scalar", 0, N // 2, N)
-        cast_w2("scalar", 1, 0, N)
-        quantize_h(0, 1, 0, HALF)
-        apply_gain(1, 0, 0, HALF)
-        bound(1, 1)
-        quantize_w2(0)
-        quantize_h(1, 0, 0, HALF)
+        quantize_h(0, 0, 0, 512)
+        cast_w2("scalar", 1, 0, 256)
+        apply_gain(0, 1, 0, 512, "vector")
+        bound(1, 0, [0, 1, 2, 3])
+        cast_w2("vector", 1, 256, 512)
+        quantize_h(0, 1, 0, 512)
+        cast_w2("scalar", 0, 256, 512)
         quantize_w2(1)
-        gate_half(0)
-        apply_gain(1, 1, 0, HALF // 2)
-        apply_gain(1, 1, HALF // 2, HALF)
-        quantize_h(1, 1, 0, HALF // 2)
-        finish(0, HALF)
-        quantize_h(1, 1, HALF // 2, HALF)
-        gate_half(1)
-        finish(HALF, HALF + HALF // 2)
-        finish(HALF + HALF // 2, S)
+        apply_gain(1, 0, 0, 512, "vector")
+        bound(1, 1, [0, 1, 2, 3])
+        quantize_w2(0)
+        quantize_h(1, 0, 0, 512)
+        gate_half(0, [0, 1, 2, 3])
+        apply_gain(1, 1, 0, 256, "vector")
+        apply_gain(1, 1, 256, 512, "vector")
+        gate_half(1, [0, 1])
+        finish(0, 512, [0])
+        quantize_h(1, 1, 0, 256)
+        finish(0, 512, [1])
+        finish(0, 512, [2])
+        gate_half(1, [2, 3])
+        quantize_h(1, 1, 256, 512)
+        finish(0, 512, [3])
+        finish(512, 768, [0])
+        finish(768, 1024, [0])
+        finish(512, 768, [2])
+        finish(768, 1024, [2])

@@ -21,8 +21,7 @@ P = 128
 PACK = 4
 PASS = P * PACK
 HALF = 512
-PIECE = 256
-SLOT = 4096
+SLOT = 8192
 
 
 def tile_list_aligned_error_gate_kernel(tc, tab_words, tab_scales, offs, w1, g, w2, wd_words, wd_scales, out):
@@ -33,18 +32,16 @@ def tile_list_aligned_error_gate_kernel(tc, tab_words, tab_scales, offs, w1, g, 
         psum = ctx.enter_context(tc.psum_pool(name="psum", bufs=1))
 
         offsets = keep.tile([P, S // 16], U16, name="offsets")
-        warm_in = stage.tile([P, 16], F32, name="warm_in", offset=4 * SLOT - 32)
-        warm_out = stage.tile([P, 16], F32, name="warm_out", offset=6 * SLOT - 32)
-        table = [stage.tile([P, T], I32, name=f"table{a}", offset=(2 * SLOT, 6 * SLOT)[a], align_bytes=64) for a in range(2)]
-        table_sc = stage.tile([P, T // 4], I32, name="table_sc", offset=8 * SLOT, align_bytes=64)
-        gain = stage.tile([P, 2, PACK], F32, name="gain", offset=8 * SLOT)
-        late = 8 * SLOT + 64
-        w1_at = {(0, 0, 0): 0, (0, 0, 1): SLOT, (1, 0, 0): 4 * SLOT, (1, 0, 1): 5 * SLOT,
-                 (0, 1, 0): late, (0, 1, 1): 4 * SLOT, (1, 1, 0): 5 * SLOT, (1, 1, 1): 2 * SLOT}
-        w2_at = {(0, 0): 3 * SLOT, (0, 1): 6 * SLOT, (1, 0): late, (1, 1): 4 * SLOT}
-        w1_raw = {k: stage.tile([P, PACK, PIECE], F32, name="w1_raw%d%d%d" % k, offset=v) for k, v in w1_at.items()}
-        w2_raw = {k: stage.tile([P, PACK, PIECE], F32, name="w2_raw%d%d" % k, offset=v) for k, v in w2_at.items()}
-        wd_codes = stage.tile([P, 2, N], I32, name="wd_codes", offset=7 * SLOT, align_bytes=64)
+        scales_at = 5 * SLOT
+        warm_in = stage.tile([P, 16], F32, name="warm_in", offset=2 * SLOT - 32)
+        warm_out = stage.tile([P, 16], F32, name="warm_out", offset=3 * SLOT)
+        table = [stage.tile([P, T], I32, name=f"table{a}", offset=(SLOT, 3 * SLOT)[a], align_bytes=64) for a in range(2)]
+        table_sc = stage.tile([P, T // 4], I32, name="table_sc", offset=scales_at, align_bytes=64)
+        gain = keep.tile([P, 2, PACK], F32, name="gain")
+        w1_at = {(0, 0): 0, (1, 0): 2 * SLOT, (0, 1): scales_at + 64 - SLOT, (1, 1): scales_at + 64 + PASS}
+        w1_raw = {k: stage.tile([P, PACK, PASS], F32, name="w1_raw%d%d" % k, offset=v) for k, v in w1_at.items()}
+        w2_raw = [stage.tile([P, PACK, N], F32, name=f"w2_raw{b}", offset=(1 + b) * SLOT) for b in range(2)]
+        wd_codes = stage.tile([P, 2, N], I32, name="wd_codes", offset=3 * SLOT, align_bytes=64)
         v_codes = [keep.tile([P, S], U32, name=f"v_codes{a}", align_bytes=64) for a in range(2)]
         picked_sc = keep.tile([P, S], U8, name="picked_sc", align_bytes=64)
         moved_sc = keep.tile([P, S // 4], I32, name="moved_sc", align_bytes=64)
@@ -53,14 +50,16 @@ def tile_list_aligned_error_gate_kernel(tc, tab_words, tab_scales, offs, w1, g, 
         w1_bf = {(a, b): keep.tile([P, PACK, P, PACK], BF16, name=f"w1_bf{a}{b}", align_bytes=64) for a in range(2) for b in range(2)}
         w2_bf = [keep.tile([P, N, PACK], BF16, name=f"w2_bf{b}", align_bytes=64) for b in range(2)]
         w1_codes = {(a, b): keep.tile([P, PASS], U32, name=f"w1_codes{a}{b}", align_bytes=64) for a in range(2) for b in range(2)}
-        w1_sc = {(a, b): keep.tile([P, PASS], U8, name=f"w1_sc{a}{b}", align_bytes=64) for a in range(2) for b in range(2)}
+        w1_sc = {(a, b): keep.tile([P, PASS], U8, name=f"w1_sc{a}{b}", align_bytes=64) for a, b in ((0, 1), (1, 0), (1, 1))}
+        w1_sc[0, 0] = stage.tile([P, PASS], U8, name="w1_sc00", offset=scales_at + 64, align_bytes=64)
         w2_codes = [keep.tile([P, N], U32, name=f"w2_codes{b}", align_bytes=64) for b in range(2)]
         w2_sc = [keep.tile([P, N], U8, name=f"w2_sc{b}", align_bytes=64) for b in range(2)]
         h_codes = [keep.tile([P, S], U32, name=f"h_codes{b}", align_bytes=64) for b in range(2)]
         h_sc = [keep.tile([P, S], U8, name=f"h_sc{b}", align_bytes=64) for b in range(2)]
         gate = keep.tile([P, N // P, S], F32, name="gate")
         bounded = {(b, s): keep.tile([P, PACK, HALF], F32, name=f"bounded{b}{s}") for b in range(2) for s in range(2)}
-        h_bf = {(b, s): keep.tile([P, HALF, PACK], BF16, name=f"h_bf{b}{s}", align_bytes=64) for b in range(2) for s in range(2)}
+        h_bf = {(b, s): keep.tile([P, HALF, PACK], BF16, name=f"h_bf{b}{s}", align_bytes=64) for b, s in ((0, 1), (1, 0), (1, 1))}
+        h_bf[0, 0] = stage.tile([P, HALF, PACK], BF16, name="h_bf00", offset=w1_at[0, 1], align_bytes=64)
         banks = [psum.tile([P, HALF], F32, name=f"bank{i}") for i in range(8)]
         results = [keep.tile([P, HALF], F32, name=f"result{i}") for i in range(8)]
         used_banks = []
@@ -80,11 +79,11 @@ def tile_list_aligned_error_gate_kernel(tc, tab_words, tab_scales, offs, w1, g, 
 
         def load_w1(a, b, c0, c1):
             rows = w1[PASS * a : PASS * (a + 1), PASS * b + c0 : PASS * b + c1]
-            nc.sync.dma_start(out=w1_raw[a, b, c0 // PIECE][:], in_=rows.rearrange("(p j) c -> p j c", j=PACK))
+            nc.sync.dma_start(out=w1_raw[a, b][:], in_=rows.rearrange("(p j) c -> p j c", j=PACK))
 
         def load_w2(b, c0, c1):
             rows = w2[PASS * b : PASS * (b + 1), c0:c1]
-            nc.sync.dma_start(out=w2_raw[b, c0 // PIECE][:], in_=rows.rearrange("(p j) c -> p j c", j=PACK))
+            nc.sync.dma_start(out=w2_raw[b][:], in_=rows.rearrange("(p j) c -> p j c", j=PACK))
 
         def load_wd():
             nc.sync.dma_start(out=wd_codes[:], in_=wd_words.rearrange("a p c i -> p a (c i)").bitcast(I32))
@@ -110,15 +109,13 @@ def tile_list_aligned_error_gate_kernel(tc, tab_words, tab_scales, offs, w1, g, 
                 nc.scalar.activation(out=dst, in_=src, func=ACT.Copy)
 
         def cast_w1(engine, a, b, m0, m1):
-            piece, c0 = divmod(PACK * m0, PIECE)
             dst = w1_bf[a, b][:, :, m0:m1, :].rearrange("p t m j -> p m j t")
-            src = w1_raw[a, b, piece][:, :, c0 : c0 + PACK * (m1 - m0)].rearrange("p j (m t) -> p m j t", t=PACK)
+            src = w1_raw[a, b][:, :, PACK * m0 : PACK * m1].rearrange("p j (m t) -> p m j t", t=PACK)
             cast(engine, dst, src)
 
         def cast_w2(engine, b, c0, c1):
-            piece, first = divmod(c0, PIECE)
             dst = w2_bf[b][:, c0:c1, :].rearrange("p (c i) j -> p c j i", i=4)
-            src = w2_raw[b, piece][:, :, first : first + c1 - c0].rearrange("p j (c i) -> p c j i", i=4)
+            src = w2_raw[b][:, :, c0:c1].rearrange("p j (c i) -> p c j i", i=4)
             cast(engine, dst, src)
 
         def quantize_w1(a, b):
@@ -186,67 +183,53 @@ def tile_list_aligned_error_gate_kernel(tc, tab_words, tab_scales, offs, w1, g, 
         nc.scalar.activation(out=warm_out[:], in_=warm_in[:], func=ACT.Sigmoid)
         for q in range(4):
             nc.gpsimd.dma_start(out=wd_sc[32 * q : 32 * q + 4, :, :], in_=wd_scales[:, 4 * q : 4 * q + 4, :].rearrange("a r c -> r a c").bitcast(I32))
-        load_w1(0, 0, 0, 256)
-        load_w1(0, 0, 256, 512)
-        load_table(0)
-        load_w1(1, 0, 0, 256)
-        load_w1(1, 0, 256, 512)
-        load_table(1)
-        cast_w1("vector", 0, 0, 0, 64)
-        cast_w1("scalar", 0, 0, 64, 128)
-        gather_scales()
-        load_w1(0, 1, 0, 256)
+        load_w1(0, 0, 0, 512)
         load_gain()
-        gather_codes(0, 0)
-        cast_w1("scalar", 1, 0, 0, 64)
-        load_w1(0, 1, 256, 512)
-        gather_codes(0, 1)
-        load_w1(1, 1, 256, 512)
-        load_w2(0, 0, 256)
-        cast_w1("scalar", 1, 0, 64, 128)
-        load_w1(1, 1, 0, 256)
+        load_table(0)
+        load_w1(1, 0, 0, 512)
+        load_table(1)
+        gather_scales()
+        load_w1(0, 1, 0, 512)
+        load_w1(1, 1, 0, 512)
+        cast_w1("scalar", 0, 0, 0, 64)
+        cast_w1("scalar", 0, 0, 64, 128)
         quantize_w1(0, 0)
+        cast_w1("vector", 1, 0, 0, 64)
+        cast_w1("scalar", 1, 0, 64, 128)
         quantize_w1(1, 0)
+        cast_w1("vector", 0, 1, 0, 64)
+        cast_w1("vector", 0, 1, 64, 128)
+        quantize_w1(0, 1)
+        gather_codes(0, 0)
         gather_codes(1, 0)
-        cast_w1("scalar", 0, 1, 0, 64)
-        load_w2(1, 0, 256)
+        gather_codes(0, 1)
         gather_codes(1, 1)
-        load_w2(0, 256, 512)
+        load_w2(0, 0, 512)
+        load_w2(1, 0, 512)
         load_wd()
         bound(0, 0, [0, 1, 2, 3])
-        cast_w1("vector", 0, 1, 64, 128)
-        load_w2(1, 256, 512)
-        cast_w1("vector", 1, 1, 64, 128)
-        quantize_w1(0, 1)
-        cast_w1("scalar", 1, 1, 0, 64)
-        cast_w2("vector", 0, 0, 256)
-        apply_gain(0, 0, 0, 512, "vector")
-        bound(0, 1, [0, 1, 2, 3])
+        cast_w1("vector", 1, 1, 0, 64)
+        cast_w1("scalar", 1, 1, 64, 128)
         quantize_w1(1, 1)
-        quantize_h(0, 0, 0, 512)
-        cast_w2("scalar", 1, 0, 256)
-        apply_gain(0, 1, 0, 512, "vector")
-        bound(1, 0, [0, 1, 2, 3])
-        cast_w2("vector", 1, 256, 512)
-        quantize_h(0, 1, 0, 512)
+        cast_w2("scalar", 0, 0, 256)
         cast_w2("scalar", 0, 256, 512)
-        quantize_w2(1)
-        apply_gain(1, 0, 0, 512, "vector")
-        bound(1, 1, [0, 1, 2, 3])
         quantize_w2(0)
+        bound(0, 1, [0, 1, 2, 3])
+        bound(1, 0, [0, 1, 2, 3])
+        cast_w2("vector", 1, 0, 256)
+        cast_w2("scalar", 1, 256, 512)
+        bound(1, 1, [0, 1, 2, 3])
+        apply_gain(0, 0, 0, 512, "vector")
+        quantize_h(0, 0, 0, 512)
+        apply_gain(0, 1, 0, 512, "vector")
+        quantize_h(0, 1, 0, 512)
+        apply_gain(1, 0, 0, 512, "vector")
+        quantize_w2(1)
         quantize_h(1, 0, 0, 512)
+        apply_gain(1, 1, 0, 512, "vector")
         gate_half(0, [0, 1, 2, 3])
-        apply_gain(1, 1, 0, 256, "vector")
-        apply_gain(1, 1, 256, 512, "vector")
-        gate_half(1, [0, 1])
+        gate_half(1, [0, 1, 2, 3])
         finish(0, 512, [0])
-        quantize_h(1, 1, 0, 256)
-        finish(0, 512, [1])
-        finish(0, 512, [2])
-        gate_half(1, [2, 3])
-        quantize_h(1, 1, 256, 512)
-        finish(0, 512, [3])
-        finish(512, 768, [0])
-        finish(768, 1024, [0])
-        finish(512, 768, [2])
-        finish(768, 1024, [2])
+        quantize_h(1, 1, 0, 512)
+        finish(0, 512, [1, 2, 3])
+        finish(512, 1024, [0, 1, 2, 3])

@@ -32,69 +32,59 @@ def tile_list_aligned_error_gate_kernel(tc, tab_words, tab_scales, offs, w1, g, 
         psum = ctx.enter_context(tc.psum_pool(name="psum", bufs=1))
 
         offsets = keep.tile([P, S // 16], U16, name="offsets")
-        scales_at = 5 * SLOT
-        warm_in = stage.tile([P, 16], F32, name="warm_in", offset=2 * SLOT - 32)
-        warm_out = stage.tile([P, 16], F32, name="warm_out", offset=3 * SLOT)
-        table = [stage.tile([P, T], I32, name=f"table{a}", offset=(SLOT, 3 * SLOT)[a], align_bytes=64) for a in range(2)]
+        scales_at = 4 * SLOT - 64
+        warm_in = keep.tile([P, 16], F32, name="warm_in")
+        warm_out = keep.tile([P, 16], F32, name="warm_out")
+        table = [stage.tile([P, T], I32, name=f"table{a}", offset=(0, 2 * SLOT)[a], align_bytes=64) for a in range(2)]
         table_sc = stage.tile([P, T // 4], I32, name="table_sc", offset=scales_at, align_bytes=64)
         gain = keep.tile([P, 2, PACK], F32, name="gain")
-        w1_at = {(0, 0): 0, (1, 0): 2 * SLOT, (0, 1): scales_at + 64 - SLOT, (1, 1): scales_at + 64 + PASS}
+        w1_at = {(0, 0): SLOT, (1, 0): 3 * SLOT, (0, 1): scales_at + T - 64, (1, 1): 0}
         w1_raw = {k: stage.tile([P, PACK, PASS], F32, name="w1_raw%d%d" % k, offset=v) for k, v in w1_at.items()}
         w2_raw = [stage.tile([P, PACK, N], F32, name=f"w2_raw{b}", offset=(1 + b) * SLOT) for b in range(2)]
         wd_codes = stage.tile([P, 2, N], I32, name="wd_codes", offset=3 * SLOT, align_bytes=64)
         v_codes = [keep.tile([P, S], U32, name=f"v_codes{a}", align_bytes=64) for a in range(2)]
         picked_sc = keep.tile([P, S], U8, name="picked_sc", align_bytes=64)
-        moved_sc = keep.tile([P, S // 4], I32, name="moved_sc", align_bytes=64)
-        v_sc = [picked_sc[:], moved_sc[:].bitcast(U8)]
+        moved_sc = [keep.tile([P, S // 4], I32, name=f"moved_sc{a}", align_bytes=64) for a in range(2)]
+        v_sc = [moved_sc[a][:].bitcast(U8) for a in range(2)]
         wd_sc = keep.tile([P, 2, N // 4], I32, name="wd_sc", align_bytes=64)
-        w1_bf = {(a, b): keep.tile([P, PACK, P, PACK], BF16, name=f"w1_bf{a}{b}", align_bytes=64) for a in range(2) for b in range(2)}
+        w1_bf = {(a, b): keep.tile([P, PACK, P, PACK], BF16, name=f"w1_bf{a}{b}", align_bytes=64) for a, b in ((0, 0), (0, 1), (1, 1))}
+        w1_pair = [keep.tile([P, 2, P, PACK], BF16, name=f"w1_pair{u}", align_bytes=64) for u in range(2)]
         w2_bf = [keep.tile([P, N, PACK], BF16, name=f"w2_bf{b}", align_bytes=64) for b in range(2)]
         w1_codes = {(a, b): keep.tile([P, PASS], U32, name=f"w1_codes{a}{b}", align_bytes=64) for a in range(2) for b in range(2)}
-        w1_sc = {(a, b): keep.tile([P, PASS], U8, name=f"w1_sc{a}{b}", align_bytes=64) for a, b in ((0, 1), (1, 0), (1, 1))}
-        w1_sc[0, 0] = stage.tile([P, PASS], U8, name="w1_sc00", offset=scales_at + 64, align_bytes=64)
+        w1_sc = {(a, b): keep.tile([P, PASS], U8, name=f"w1_sc{a}{b}", align_bytes=64) for a in range(2) for b in range(2)}
         w2_codes = [keep.tile([P, N], U32, name=f"w2_codes{b}", align_bytes=64) for b in range(2)]
         w2_sc = [keep.tile([P, N], U8, name=f"w2_sc{b}", align_bytes=64) for b in range(2)]
         h_codes = [keep.tile([P, S], U32, name=f"h_codes{b}", align_bytes=64) for b in range(2)]
         h_sc = [keep.tile([P, S], U8, name=f"h_sc{b}", align_bytes=64) for b in range(2)]
         gate = keep.tile([P, N // P, S], F32, name="gate")
-        bounded = {(b, s): keep.tile([P, PACK, HALF], F32, name=f"bounded{b}{s}") for b in range(2) for s in range(2)}
-        h_bf = {(b, s): keep.tile([P, HALF, PACK], BF16, name=f"h_bf{b}{s}", align_bytes=64) for b, s in ((0, 1), (1, 0), (1, 1))}
-        h_bf[0, 0] = stage.tile([P, HALF, PACK], BF16, name="h_bf00", offset=w1_at[0, 1], align_bytes=64)
+        bounded = {(b, s): keep.tile([P, PACK, HALF], F32, name=f"bounded{b}{s}") for b, s in ((0, 0), (0, 1), (1, 1))}
+        bounded[1, 0] = stage.tile([P, PACK, HALF], F32, name="bounded10", offset=SLOT)
+        QUART = HALF // 2
+        h_bf = {(b, s, u): keep.tile([P, QUART, PACK], BF16, name=f"h_bf{b}{s}{u}", align_bytes=64)
+                for b in range(2) for s in range(2) for u in range(2) if b == 1}
+        for s in range(2):
+            for u in range(2):
+                h_bf[0, s, u] = stage.tile([P, QUART, PACK], BF16, name=f"h_bf0{s}{u}", offset=2048 * (2 * s + u), align_bytes=64)
         banks = [psum.tile([P, HALF], F32, name=f"bank{i}") for i in range(8)]
         results = [keep.tile([P, HALF], F32, name=f"result{i}") for i in range(8)]
-        used_banks = []
-        used_results = []
-
-        def next_bank():
-            used_banks.append(len(used_banks) % len(banks))
-            return banks[used_banks[-1]]
 
         def load_table_scales():
-            for q in range(4):
-                nc.sync.dma_start(out=table_sc[32 * q : 32 * q + 4, :], in_=tab_scales[0, 4 * q : 4 * q + 4, :].bitcast(I32))
-            nc.sync.dma_start(out=table_sc[8:24, :], in_=tab_scales[1].bitcast(I32))
+            nc.sync.dma_start(out=table_sc[0:32, :], in_=tab_scales.rearrange("a q t -> (a q) t").bitcast(I32))
 
         def load_table(a):
             nc.sync.dma_start(out=table[a][:], in_=tab_words[a].rearrange("p t i -> p (t i)").bitcast(I32))
 
-        def load_w1(a, b, c0, c1):
-            rows = w1[PASS * a : PASS * (a + 1), PASS * b + c0 : PASS * b + c1]
+        def load_w1(a, b):
+            rows = w1[PASS * a : PASS * (a + 1), PASS * b : PASS * (b + 1)]
             nc.sync.dma_start(out=w1_raw[a, b][:], in_=rows.rearrange("(p j) c -> p j c", j=PACK))
 
-        def load_w2(b, c0, c1):
-            rows = w2[PASS * b : PASS * (b + 1), c0:c1]
+        def load_w2(b):
+            rows = w2[PASS * b : PASS * (b + 1), :]
             nc.sync.dma_start(out=w2_raw[b][:], in_=rows.rearrange("(p j) c -> p j c", j=PACK))
 
-        def load_wd():
-            nc.sync.dma_start(out=wd_codes[:], in_=wd_words.rearrange("a p c i -> p a (c i)").bitcast(I32))
-
-        def load_gain():
-            nc.sync.dma_start(out=gain[:], in_=g.rearrange("(b p t) -> p b t", b=2, t=PACK))
-
-        def gather_scales():
-            nc.vector.tensor_copy(picked_sc[:], table_sc[:].bitcast(U8).indirect(offsets[:]))
+        def move_scales(a):
             for q in range(4):
-                nc.sync.dma_start(out=moved_sc[32 * q : 32 * q + 4, :], in_=picked_sc[8 + 4 * q : 12 + 4 * q, :].bitcast(I32))
+                nc.sync.dma_start(out=moved_sc[a][32 * q : 32 * q + 4, :], in_=picked_sc[16 * a + 4 * q : 16 * a + 4 * q + 4, :].bitcast(I32))
 
         def gather_codes(a, s):
             window = table[a][:].bitcast(U32).indirect(offsets[:, 32 * s : 32 * (s + 1)])
@@ -103,14 +93,17 @@ def tile_list_aligned_error_gate_kernel(tc, tab_words, tab_scales, offs, w1, g, 
         def cast(engine, dst, src):
             if engine == "vector":
                 nc.vector.tensor_copy(out=dst, in_=src)
-            elif engine == "gpsimd":
-                nc.gpsimd.tensor_scalar(out=dst, in0=src, scalar1=1.0, scalar2=0.0, op0=MULT, op1=ADD)
             else:
                 nc.scalar.activation(out=dst, in_=src, func=ACT.Copy)
 
         def cast_w1(engine, a, b, m0, m1):
             dst = w1_bf[a, b][:, :, m0:m1, :].rearrange("p t m j -> p m j t")
             src = w1_raw[a, b][:, :, PACK * m0 : PACK * m1].rearrange("p j (m t) -> p m j t", t=PACK)
+            cast(engine, dst, src)
+
+        def cast_pair(engine, u):
+            dst = w1_pair[u][:].rearrange("p t m j -> p m j t")
+            src = w1_raw[1, 0][:].rearrange("p j (m t) -> p m j t", t=PACK)[:, :, :, 2 * u : 2 * u + 2]
             cast(engine, dst, src)
 
         def cast_w2(engine, b, c0, c1):
@@ -121,115 +114,143 @@ def tile_list_aligned_error_gate_kernel(tc, tab_words, tab_scales, offs, w1, g, 
         def quantize_w1(a, b):
             nc.vector.quantize_mx(out=w1_codes[a, b][:].bitcast(E4M3), scales=w1_sc[a, b][:], in_=w1_bf[a, b][:].rearrange("p t m j -> p (t m j)"))
 
+        def quantize_pair(u):
+            cols = slice(2 * P * u, 2 * P * (u + 1))
+            nc.vector.quantize_mx(out=w1_codes[1, 0][:, cols].bitcast(E4M3), scales=w1_sc[1, 0][:, cols], in_=w1_pair[u][:].rearrange("p t m j -> p (t m j)"))
+
         def quantize_w2(b):
             nc.vector.quantize_mx(out=w2_codes[b][:].bitcast(E4M3), scales=w2_sc[b][:], in_=w2_bf[b][:].rearrange("p c j -> p (c j)"))
 
-        def table_product(codes, scales, s):
+        def table_pass(bank, codes, scales, a, s):
             cols = slice(HALF * s, HALF * (s + 1))
-            acc = next_bank()
+            nc.tensor.matmul_mx(out=banks[bank][:], lhsT=codes.bitcast(E4M3), lhsT_scale=scales,
+                                rhs=v_codes[a][:, cols].bitcast(E5M2), rhs_scale=v_sc[a][:, cols],
+                                start=(a == 0), stop=(a == 1))
+
+        def w1_pass(a, b, s, t):
+            cols = slice(P * t, P * (t + 1))
+            table_pass(4 * s + t, w1_codes[a, b][:, cols], w1_sc[a, b][:, cols], a, s)
+
+        def bound(b, s, t):
+            nc.scalar.activation(out=bounded[b, s][:, t, :], in_=banks[4 * s + t][:], func=ACT.Tanh)
+
+        def direct(s, n):
+            cols = slice(P * n, P * (n + 1))
             for a in range(2):
-                nc.tensor.matmul_mx(out=acc[:], lhsT=codes[a].bitcast(E4M3), lhsT_scale=scales[a],
-                                    rhs=v_codes[a][:, cols].bitcast(E5M2), rhs_scale=v_sc[a][:, cols],
-                                    start=(a == 0), stop=(a == 1))
-            return acc
+                table_pass(4 * s + n, wd_codes[:, a, cols], wd_sc[:, a, :].bitcast(U8)[:, cols], a, s)
 
-        def bound(b, s, slots):
-            for t in slots:
-                cols = slice(P * t, P * (t + 1))
-                acc = table_product([w1_codes[a, b][:, cols] for a in range(2)], [w1_sc[a, b][:, cols] for a in range(2)], s)
-                nc.scalar.activation(out=bounded[b, s][:, t, :], in_=acc[:], func=ACT.Tanh)
+        def make_gate(s, n):
+            nc.scalar.activation(out=gate[:, n, HALF * s : HALF * (s + 1)], in_=banks[4 * s + n][:], func=ACT.Sigmoid)
 
-        def gate_half(s, tiles):
-            for n in tiles:
-                cols = slice(P * n, P * (n + 1))
-                acc = table_product([wd_codes[:, a, cols] for a in range(2)], [wd_sc[:, a, :].bitcast(U8)[:, cols] for a in range(2)], s)
-                nc.scalar.activation(out=gate[:, n, HALF * s : HALF * (s + 1)], in_=acc[:], func=ACT.Sigmoid)
-
-        def apply_gain(b, s, c0, c1, engine):
-            factors = gain[:, b, :]
-            (nc.vector if engine == "vector" else nc.gpsimd).tensor_tensor(
-                out=h_bf[b, s][:, c0:c1, :].rearrange("p (c i) t -> p c t i", i=4),
-                in0=bounded[b, s][:, :, c0:c1].rearrange("p t (c i) -> p c t i", i=4),
-                in1=factors.unsqueeze(1).unsqueeze(3).to_broadcast([P, (c1 - c0) // 4, PACK, 4]),
+        def apply_gain(b, s, u):
+            nc.vector.tensor_tensor(
+                out=h_bf[b, s, u][:].rearrange("p (c i) t -> p c t i", i=4),
+                in0=bounded[b, s][:, :, QUART * u : QUART * (u + 1)].rearrange("p t (c i) -> p c t i", i=4),
+                in1=gain[:, b, :].unsqueeze(1).unsqueeze(3).to_broadcast([P, QUART // 4, PACK, 4]),
                 op=MULT,
             )
 
-        def quantize_h(b, s, c0, c1):
-            cols = slice(HALF * s + c0, HALF * s + c1)
-            nc.vector.quantize_mx(out=h_codes[b][:, cols].bitcast(E4M3), scales=h_sc[b][:, cols], in_=h_bf[b, s][:, c0:c1, :].rearrange("p c t -> p (c t)"))
+        def quantize_h(b, s, u):
+            cols = slice(HALF * s + QUART * u, HALF * s + QUART * (u + 1))
+            nc.vector.quantize_mx(out=h_codes[b][:, cols].bitcast(E4M3), scales=h_sc[b][:, cols], in_=h_bf[b, s, u][:].rearrange("p c t -> p (c t)"))
 
-        def finish(c0, c1, firsts):
-            cols = slice(c0, c1)
-            tiles = HALF // (c1 - c0)
-            for n0 in firsts:
-                y = next_bank()[:].rearrange("p (i s) -> p i s", i=tiles)
-                for i in range(tiles):
-                    rows = slice(P * (n0 + i), P * (n0 + i + 1))
-                    for b in range(2):
-                        nc.tensor.matmul_mx(out=y[:, i, :], lhsT=w2_codes[b][:, rows].bitcast(E4M3), lhsT_scale=w2_sc[b][:, rows],
-                                            rhs=h_codes[b][:, cols].bitcast(E4M3), rhs_scale=h_sc[b][:, cols],
-                                            start=(b == 0), stop=(b == 1))
-                used_results.append(n0)
-                result = results[len(used_results) - 1][:].rearrange("p (i s) -> p i s", i=tiles)
-                nc.vector.tensor_tensor(out=result, in0=y, in1=gate[:, n0 : n0 + tiles, cols], op=MULT)
-                nc.sync.dma_start(out=out[P * n0 : P * (n0 + tiles), cols].rearrange("(i p) s -> p i s", p=P), in_=result)
+        def w2_pass(b, s, n, bank):
+            cols = slice(HALF * s, HALF * (s + 1))
+            rows = slice(P * n, P * (n + 1))
+            nc.tensor.matmul_mx(out=banks[bank][:], lhsT=w2_codes[b][:, rows].bitcast(E4M3), lhsT_scale=w2_sc[b][:, rows],
+                                rhs=h_codes[b][:, cols].bitcast(E4M3), rhs_scale=h_sc[b][:, cols],
+                                start=(b == 0), stop=(b == 1))
+
+        def finish(s, n, bank):
+            cols = slice(HALF * s, HALF * (s + 1))
+            result = results[4 * s + n]
+            nc.vector.tensor_tensor(out=result[:], in0=banks[bank][:], in1=gate[:, n, cols], op=MULT)
+            nc.sync.dma_start(out=out[P * n : P * (n + 1), cols], in_=result[:])
 
         nc.sync.dma_start(offsets[:], offs)
-        nc.vector.memset(table_sc[:], 0)
-        nc.gpsimd.memset(warm_in[:], 0.0)
-        nc.gpsimd.memset(wd_sc[:], 0)
-        nc.gpsimd.memset(moved_sc[:], 0)
         load_table_scales()
+        nc.gpsimd.memset(warm_in[:], 0.0)
+        nc.vector.memset(table_sc[32:64, :], 0)
+        nc.vector.memset(table_sc[64:128, :], 0)
         nc.scalar.activation(out=warm_out[:], in_=warm_in[:], func=ACT.Sigmoid)
+        nc.gpsimd.memset(moved_sc[0][:], 0)
+        nc.gpsimd.memset(moved_sc[1][:], 0)
+        nc.gpsimd.memset(wd_sc[:], 0)
+        nc.gpsimd.dma_start(out=gain[:], in_=g.rearrange("(b p t) -> p b t", b=2, t=PACK))
         for q in range(4):
             nc.gpsimd.dma_start(out=wd_sc[32 * q : 32 * q + 4, :, :], in_=wd_scales[:, 4 * q : 4 * q + 4, :].rearrange("a r c -> r a c").bitcast(I32))
-        load_w1(0, 0, 0, 512)
-        load_gain()
         load_table(0)
-        load_w1(1, 0, 0, 512)
+        load_w1(0, 0)
         load_table(1)
-        gather_scales()
-        load_w1(0, 1, 0, 512)
-        load_w1(1, 1, 0, 512)
-        cast_w1("scalar", 0, 0, 0, 64)
-        cast_w1("scalar", 0, 0, 64, 128)
-        quantize_w1(0, 0)
-        cast_w1("vector", 1, 0, 0, 64)
-        cast_w1("scalar", 1, 0, 64, 128)
-        quantize_w1(1, 0)
-        cast_w1("vector", 0, 1, 0, 64)
-        cast_w1("vector", 0, 1, 64, 128)
-        quantize_w1(0, 1)
+        nc.vector.tensor_copy(picked_sc[:], table_sc[:].bitcast(U8).indirect(offsets[:]))
+        move_scales(0)
+        load_w1(1, 0)
+        move_scales(1)
+        load_w1(0, 1)
         gather_codes(0, 0)
-        gather_codes(1, 0)
         gather_codes(0, 1)
+        load_w1(1, 1)
+        cast_w1("scalar", 0, 0, 0, 64)
+        cast_w1("vector", 0, 0, 64, 128)
+        load_w2(0)
+        quantize_w1(0, 0)
+        for s in range(2):
+            for t in range(PACK):
+                w1_pass(0, 0, s, t)
+        gather_codes(1, 0)
         gather_codes(1, 1)
-        load_w2(0, 0, 512)
-        load_w2(1, 0, 512)
-        load_wd()
-        bound(0, 0, [0, 1, 2, 3])
-        cast_w1("vector", 1, 1, 0, 64)
-        cast_w1("scalar", 1, 1, 64, 128)
+        load_w2(1)
+        cast_pair("vector", 0)
+        cast_pair("scalar", 1)
+        nc.sync.dma_start(out=wd_codes[:], in_=wd_words.rearrange("a p c i -> p a (c i)").bitcast(I32))
+        quantize_pair(0)
+        quantize_pair(1)
+        for s in range(2):
+            for t in range(PACK):
+                w1_pass(1, 0, s, t)
+                bound(0, s, t)
+        cast_w1("vector", 0, 1, 0, 128)
+        quantize_w1(0, 1)
+        cast_w1("vector", 1, 1, 0, 128)
+        apply_gain(0, 0, 0)
         quantize_w1(1, 1)
-        cast_w2("scalar", 0, 0, 256)
-        cast_w2("scalar", 0, 256, 512)
+        cast_w2("scalar", 0, 0, 512)
+        for s in range(2):
+            for t in range(PACK):
+                w1_pass(0, 1, s, t)
+            for t in range(PACK):
+                w1_pass(1, 1, s, t)
+                bound(1, s, t)
+        apply_gain(0, 0, 1)
+        quantize_h(0, 0, 0)
+        apply_gain(0, 1, 0)
+        quantize_h(0, 0, 1)
+        apply_gain(0, 1, 1)
+        quantize_h(0, 1, 0)
+        cast_w2("scalar", 1, 0, 512)
+        for s in range(2):
+            for n in range(4):
+                direct(s, n)
+        apply_gain(1, 0, 0)
+        quantize_h(0, 1, 1)
+        apply_gain(1, 0, 1)
+        quantize_h(1, 0, 0)
         quantize_w2(0)
-        bound(0, 1, [0, 1, 2, 3])
-        bound(1, 0, [0, 1, 2, 3])
-        cast_w2("vector", 1, 0, 256)
-        cast_w2("scalar", 1, 256, 512)
-        bound(1, 1, [0, 1, 2, 3])
-        apply_gain(0, 0, 0, 512, "vector")
-        quantize_h(0, 0, 0, 512)
-        apply_gain(0, 1, 0, 512, "vector")
-        quantize_h(0, 1, 0, 512)
-        apply_gain(1, 0, 0, 512, "vector")
+        quantize_h(1, 0, 1)
+        apply_gain(1, 1, 0)
         quantize_w2(1)
-        quantize_h(1, 0, 0, 512)
-        apply_gain(1, 1, 0, 512, "vector")
-        gate_half(0, [0, 1, 2, 3])
-        gate_half(1, [0, 1, 2, 3])
-        finish(0, 512, [0])
-        quantize_h(1, 1, 0, 512)
-        finish(0, 512, [1, 2, 3])
-        finish(512, 1024, [0, 1, 2, 3])
+        for n in range(4):
+            make_gate(0, n)
+            w2_pass(0, 0, n, n)
+            w2_pass(1, 0, n, n)
+        apply_gain(1, 1, 1)
+        quantize_h(1, 1, 0)
+        finish(0, 0, 0)
+        quantize_h(1, 1, 1)
+        for n in range(1, 4):
+            finish(0, n, n)
+        for n in range(4):
+            make_gate(1, n)
+            w2_pass(0, 1, n, n)
+            w2_pass(1, 1, n, n)
+            finish(1, n, n)

@@ -46,25 +46,22 @@ def tile_list_aligned_error_gate_kernel(tc, tab_words, tab_scales, offs, w1, g, 
         picked_sc = keep.tile([P, S], U8, name="picked_sc", align_bytes=64)
         moved_sc = [keep.tile([P, S // 4], I32, name=f"moved_sc{a}", align_bytes=64) for a in range(2)]
         v_sc = [moved_sc[a][:].bitcast(U8) for a in range(2)]
-        wd_sc = keep.tile([P, 2, N // 4], I32, name="wd_sc", align_bytes=64)
+        wd_sc = stage.tile([P, 2, N // 4], I32, name="wd_sc", offset=3 * SLOT + 4096, align_bytes=64)
         w1_bf = {(a, b): keep.tile([P, PACK, P, PACK], BF16, name=f"w1_bf{a}{b}", align_bytes=64) for a, b in ((0, 0), (0, 1), (1, 1))}
         w1_pair = [keep.tile([P, 2, P, PACK], BF16, name=f"w1_pair{u}", align_bytes=64) for u in range(2)]
-        w2_bf = [keep.tile([P, N, PACK], BF16, name=f"w2_bf{b}", align_bytes=64) for b in range(2)]
+        w2_bf = [keep.tile([P, N * PACK], BF16, name=f"w2_bf{b}", align_bytes=64) for b in range(2)]
         w1_codes = {(a, b): keep.tile([P, PASS], U32, name=f"w1_codes{a}{b}", align_bytes=64) for a in range(2) for b in range(2)}
         w1_sc = {(a, b): keep.tile([P, PASS], U8, name=f"w1_sc{a}{b}", align_bytes=64) for a in range(2) for b in range(2)}
-        w2_codes = [keep.tile([P, N], U32, name=f"w2_codes{b}", align_bytes=64) for b in range(2)]
-        w2_sc = [keep.tile([P, N], U8, name=f"w2_sc{b}", align_bytes=64) for b in range(2)]
+        w2_codes = keep.tile([P, 2 * N], U32, name="w2_codes", align_bytes=64)
+        w2_sc = keep.tile([P, 2 * N], U8, name="w2_sc", align_bytes=64)
         h_codes = [keep.tile([P, S], U32, name=f"h_codes{b}", align_bytes=64) for b in range(2)]
         h_sc = [keep.tile([P, S], U8, name=f"h_sc{b}", align_bytes=64) for b in range(2)]
         gate = keep.tile([P, N // P, S], F32, name="gate")
         bounded = {(b, s): keep.tile([P, PACK, HALF], F32, name=f"bounded{b}{s}") for b, s in ((0, 0), (0, 1), (1, 1))}
         bounded[1, 0] = stage.tile([P, PACK, HALF], F32, name="bounded10", offset=SLOT)
-        QUART = HALF // 2
-        h_bf = {(b, s, u): keep.tile([P, QUART, PACK], BF16, name=f"h_bf{b}{s}{u}", align_bytes=64)
-                for b in range(2) for s in range(2) for u in range(2) if b == 1}
+        h_bf = {(1, s): keep.tile([P, HALF, PACK], BF16, name=f"h_bf1{s}", align_bytes=64) for s in range(2)}
         for s in range(2):
-            for u in range(2):
-                h_bf[0, s, u] = stage.tile([P, QUART, PACK], BF16, name=f"h_bf0{s}{u}", offset=2048 * (2 * s + u), align_bytes=64)
+            h_bf[0, s] = stage.tile([P, HALF, PACK], BF16, name=f"h_bf0{s}", offset=w1_at[s, 1], align_bytes=64)
         banks = [psum.tile([P, HALF], F32, name=f"bank{i}") for i in range(8)]
         results = [keep.tile([P, HALF], F32, name=f"result{i}") for i in range(8)]
 
@@ -107,7 +104,7 @@ def tile_list_aligned_error_gate_kernel(tc, tab_words, tab_scales, offs, w1, g, 
             cast(engine, dst, src)
 
         def cast_w2(engine, b, c0, c1):
-            dst = w2_bf[b][:, c0:c1, :].rearrange("p (c i) j -> p c j i", i=4)
+            dst = w2_bf[b][:, PACK * c0 : PACK * c1].rearrange("p (c i j) -> p c j i", i=4, j=PACK)
             src = w2_raw[b][:, :, c0:c1].rearrange("p j (c i) -> p c j i", i=4)
             cast(engine, dst, src)
 
@@ -119,7 +116,8 @@ def tile_list_aligned_error_gate_kernel(tc, tab_words, tab_scales, offs, w1, g, 
             nc.vector.quantize_mx(out=w1_codes[1, 0][:, cols].bitcast(E4M3), scales=w1_sc[1, 0][:, cols], in_=w1_pair[u][:].rearrange("p t m j -> p (t m j)"))
 
         def quantize_w2(b):
-            nc.vector.quantize_mx(out=w2_codes[b][:].bitcast(E4M3), scales=w2_sc[b][:], in_=w2_bf[b][:].rearrange("p c j -> p (c j)"))
+            cols = slice(N * b, N * (b + 1))
+            nc.vector.quantize_mx(out=w2_codes[:, cols].bitcast(E4M3), scales=w2_sc[:, cols], in_=w2_bf[b][:])
 
         def table_pass(bank, codes, scales, a, s):
             cols = slice(HALF * s, HALF * (s + 1))
@@ -142,22 +140,22 @@ def tile_list_aligned_error_gate_kernel(tc, tab_words, tab_scales, offs, w1, g, 
         def make_gate(s, n):
             nc.scalar.activation(out=gate[:, n, HALF * s : HALF * (s + 1)], in_=banks[4 * s + n][:], func=ACT.Sigmoid)
 
-        def apply_gain(b, s, u):
+        def apply_gain(b, s):
             nc.vector.tensor_tensor(
-                out=h_bf[b, s, u][:].rearrange("p (c i) t -> p c t i", i=4),
-                in0=bounded[b, s][:, :, QUART * u : QUART * (u + 1)].rearrange("p t (c i) -> p c t i", i=4),
-                in1=gain[:, b, :].unsqueeze(1).unsqueeze(3).to_broadcast([P, QUART // 4, PACK, 4]),
+                out=h_bf[b, s][:].rearrange("p (c i) t -> p c t i", i=4),
+                in0=bounded[b, s][:].rearrange("p t (c i) -> p c t i", i=4),
+                in1=gain[:, b, :].unsqueeze(1).unsqueeze(3).to_broadcast([P, HALF // 4, PACK, 4]),
                 op=MULT,
             )
 
-        def quantize_h(b, s, u):
-            cols = slice(HALF * s + QUART * u, HALF * s + QUART * (u + 1))
-            nc.vector.quantize_mx(out=h_codes[b][:, cols].bitcast(E4M3), scales=h_sc[b][:, cols], in_=h_bf[b, s, u][:].rearrange("p c t -> p (c t)"))
+        def quantize_h(b, s):
+            cols = slice(HALF * s, HALF * (s + 1))
+            nc.vector.quantize_mx(out=h_codes[b][:, cols].bitcast(E4M3), scales=h_sc[b][:, cols], in_=h_bf[b, s][:].rearrange("p c t -> p (c t)"))
 
         def w2_pass(b, s, n, bank):
             cols = slice(HALF * s, HALF * (s + 1))
-            rows = slice(P * n, P * (n + 1))
-            nc.tensor.matmul_mx(out=banks[bank][:], lhsT=w2_codes[b][:, rows].bitcast(E4M3), lhsT_scale=w2_sc[b][:, rows],
+            rows = slice(N * b + P * n, N * b + P * (n + 1))
+            nc.tensor.matmul_mx(out=banks[bank][:], lhsT=w2_codes[:, rows].bitcast(E4M3), lhsT_scale=w2_sc[:, rows],
                                 rhs=h_codes[b][:, cols].bitcast(E4M3), rhs_scale=h_sc[b][:, cols],
                                 start=(b == 0), stop=(b == 1))
 
@@ -170,15 +168,12 @@ def tile_list_aligned_error_gate_kernel(tc, tab_words, tab_scales, offs, w1, g, 
         nc.sync.dma_start(offsets[:], offs)
         load_table_scales()
         nc.gpsimd.memset(warm_in[:], 0.0)
-        nc.vector.memset(table_sc[32:64, :], 0)
+        nc.gpsimd.memset(table_sc[32:64, :], 0)
         nc.vector.memset(table_sc[64:128, :], 0)
         nc.scalar.activation(out=warm_out[:], in_=warm_in[:], func=ACT.Sigmoid)
         nc.gpsimd.memset(moved_sc[0][:], 0)
         nc.gpsimd.memset(moved_sc[1][:], 0)
-        nc.gpsimd.memset(wd_sc[:], 0)
         nc.gpsimd.dma_start(out=gain[:], in_=g.rearrange("(b p t) -> p b t", b=2, t=PACK))
-        for q in range(4):
-            nc.gpsimd.dma_start(out=wd_sc[32 * q : 32 * q + 4, :, :], in_=wd_scales[:, 4 * q : 4 * q + 4, :].rearrange("a r c -> r a c").bitcast(I32))
         load_table(0)
         load_w1(0, 0)
         load_table(1)
@@ -187,8 +182,7 @@ def tile_list_aligned_error_gate_kernel(tc, tab_words, tab_scales, offs, w1, g, 
         load_w1(1, 0)
         move_scales(1)
         load_w1(0, 1)
-        gather_codes(0, 0)
-        gather_codes(0, 1)
+        nc.vector.tensor_copy(v_codes[0][:], table[0][:].bitcast(U32).indirect(offsets[:]))
         load_w1(1, 1)
         cast_w1("scalar", 0, 0, 0, 64)
         cast_w1("vector", 0, 0, 64, 128)
@@ -202,7 +196,10 @@ def tile_list_aligned_error_gate_kernel(tc, tab_words, tab_scales, offs, w1, g, 
         load_w2(1)
         cast_pair("vector", 0)
         cast_pair("scalar", 1)
+        nc.gpsimd.memset(wd_sc[:], 0)
         nc.sync.dma_start(out=wd_codes[:], in_=wd_words.rearrange("a p c i -> p a (c i)").bitcast(I32))
+        for q in range(4):
+            nc.sync.dma_start(out=wd_sc[32 * q : 32 * q + 4, :, :], in_=wd_scales[:, 4 * q : 4 * q + 4, :].rearrange("a r c -> r a c").bitcast(I32))
         quantize_pair(0)
         quantize_pair(1)
         for s in range(2):
@@ -211,8 +208,9 @@ def tile_list_aligned_error_gate_kernel(tc, tab_words, tab_scales, offs, w1, g, 
                 bound(0, s, t)
         cast_w1("vector", 0, 1, 0, 128)
         quantize_w1(0, 1)
+        apply_gain(0, 0)
         cast_w1("vector", 1, 1, 0, 128)
-        apply_gain(0, 0, 0)
+        quantize_h(0, 0)
         quantize_w1(1, 1)
         cast_w2("scalar", 0, 0, 512)
         for s in range(2):
@@ -221,33 +219,23 @@ def tile_list_aligned_error_gate_kernel(tc, tab_words, tab_scales, offs, w1, g, 
             for t in range(PACK):
                 w1_pass(1, 1, s, t)
                 bound(1, s, t)
-        apply_gain(0, 0, 1)
-        quantize_h(0, 0, 0)
-        apply_gain(0, 1, 0)
-        quantize_h(0, 0, 1)
-        apply_gain(0, 1, 1)
-        quantize_h(0, 1, 0)
+        apply_gain(0, 1)
+        quantize_w2(0)
+        quantize_h(0, 1)
         cast_w2("scalar", 1, 0, 512)
         for s in range(2):
             for n in range(4):
                 direct(s, n)
-        apply_gain(1, 0, 0)
-        quantize_h(0, 1, 1)
-        apply_gain(1, 0, 1)
-        quantize_h(1, 0, 0)
-        quantize_w2(0)
-        quantize_h(1, 0, 1)
-        apply_gain(1, 1, 0)
+        apply_gain(1, 0)
+        apply_gain(1, 1)
+        quantize_h(1, 0)
         quantize_w2(1)
         for n in range(4):
             make_gate(0, n)
             w2_pass(0, 0, n, n)
             w2_pass(1, 0, n, n)
-        apply_gain(1, 1, 1)
-        quantize_h(1, 1, 0)
-        finish(0, 0, 0)
-        quantize_h(1, 1, 1)
-        for n in range(1, 4):
+        quantize_h(1, 1)
+        for n in range(4):
             finish(0, n, n)
         for n in range(4):
             make_gate(1, n)

@@ -1,6 +1,7 @@
 from contextlib import ExitStack
 
 import concourse.mybir as mybir
+from concourse.masks import make_identity
 
 K, T, S, H, N = 1024, 2048, 1024, 1024, 512
 FLOPS = 2 * S * (K * H + H * N + K * N)
@@ -32,37 +33,46 @@ def tile_list_aligned_error_gate_kernel(tc, tab_words, tab_scales, offs, w1, g, 
         psum = ctx.enter_context(tc.psum_pool(name="psum", bufs=1))
 
         offsets = keep.tile([P, S // 16], U16, name="offsets")
-        scales_at = 4 * SLOT - 64
+        scales_at = 2 * SLOT - 64
         warm_in = keep.tile([P, 16], F32, name="warm_in")
         warm_out = keep.tile([P, 16], F32, name="warm_out")
-        table = [stage.tile([P, T], I32, name=f"table{a}", offset=(0, 2 * SLOT)[a], align_bytes=64) for a in range(2)]
+        table = [stage.tile([P, T], I32, name=f"table{a}", offset=(0, 5 * SLOT)[a], align_bytes=64) for a in range(2)]
         table_sc = stage.tile([P, T // 4], I32, name="table_sc", offset=scales_at, align_bytes=64)
         gain = keep.tile([P, 2, PACK], F32, name="gain")
-        w1_at = {(0, 0): SLOT, (1, 0): 3 * SLOT, (0, 1): scales_at + T - 64, (1, 1): 0}
+        gain_rows = keep.tile([P, PASS], F32, name="gain_rows")
+        ident = keep.tile([P, P], F32, name="ident")
+        gain_ps = psum.tile([P, P, PACK], F32, name="gain_ps")
+        w1_at = {(0, 0): 4 * SLOT, (1, 0): scales_at + T - 64, (0, 1): SLOT, (1, 1): 0}
         w1_raw = {k: stage.tile([P, PACK, PASS], F32, name="w1_raw%d%d" % k, offset=v) for k, v in w1_at.items()}
-        w2_raw = [stage.tile([P, PACK, N], F32, name=f"w2_raw{b}", offset=(1 + b) * SLOT) for b in range(2)]
-        wd_codes = stage.tile([P, 2, N], I32, name="wd_codes", offset=3 * SLOT, align_bytes=64)
+        w2_raw = [stage.tile([P, PACK, N], F32, name=f"w2_raw{b}", offset=(4 + b) * SLOT) for b in range(2)]
+        wd_codes = stage.tile([P, 2, N], I32, name="wd_codes", offset=w1_at[1, 0], align_bytes=64)
         v_codes = [keep.tile([P, S], U32, name=f"v_codes{a}", align_bytes=64) for a in range(2)]
         picked_sc = keep.tile([P, S], U8, name="picked_sc", align_bytes=64)
         moved_sc = [keep.tile([P, S // 4], I32, name=f"moved_sc{a}", align_bytes=64) for a in range(2)]
         v_sc = [moved_sc[a][:].bitcast(U8) for a in range(2)]
-        wd_sc = stage.tile([P, 2, N // 4], I32, name="wd_sc", offset=3 * SLOT + 4096, align_bytes=64)
+        wd_sc = stage.tile([P, 2, N // 4], I32, name="wd_sc", offset=w1_at[1, 0] + 4096, align_bytes=64)
         w1_bf = {(a, b): keep.tile([P, PACK, P, PACK], BF16, name=f"w1_bf{a}{b}", align_bytes=64) for a, b in ((0, 0), (0, 1), (1, 1))}
         w1_pair = [keep.tile([P, 2, P, PACK], BF16, name=f"w1_pair{u}", align_bytes=64) for u in range(2)]
-        w2_bf = [keep.tile([P, N * PACK], BF16, name=f"w2_bf{b}", align_bytes=64) for b in range(2)]
+        w2_bf = [keep.tile([P, N * PACK], BF16, name="w2_bf0", align_bytes=64),
+                 stage.tile([P, N * PACK], BF16, name="w2_bf1", offset=6 * SLOT, align_bytes=64)]
         w1_codes = {(a, b): keep.tile([P, PASS], U32, name=f"w1_codes{a}{b}", align_bytes=64) for a in range(2) for b in range(2)}
         w1_sc = {(a, b): keep.tile([P, PASS], U8, name=f"w1_sc{a}{b}", align_bytes=64) for a in range(2) for b in range(2)}
         w2_codes = keep.tile([P, 2 * N], U32, name="w2_codes", align_bytes=64)
         w2_sc = keep.tile([P, 2 * N], U8, name="w2_sc", align_bytes=64)
-        h_codes = [keep.tile([P, S], U32, name=f"h_codes{b}", align_bytes=64) for b in range(2)]
-        h_sc = [keep.tile([P, S], U8, name=f"h_sc{b}", align_bytes=64) for b in range(2)]
+        h_codes = {(b, s): keep.tile([P, HALF], U32, name=f"h_codes{b}{s}", align_bytes=64) for b, s in ((0, 0), (1, 0), (1, 1))}
+        h_codes[0, 1] = stage.tile([P, HALF], U32, name="h_codes01", offset=5 * SLOT, align_bytes=64)
+        h_sc = [stage.tile([P, S], U8, name="h_sc0", offset=w1_at[1, 1], align_bytes=64), keep.tile([P, S], U8, name="h_sc1", align_bytes=64)]
         gate = keep.tile([P, N // P, S], F32, name="gate")
         bounded = {(b, s): keep.tile([P, PACK, HALF], F32, name=f"bounded{b}{s}") for b, s in ((0, 0), (0, 1), (1, 1))}
-        bounded[1, 0] = stage.tile([P, PACK, HALF], F32, name="bounded10", offset=SLOT)
-        h_bf = {(1, s): keep.tile([P, HALF, PACK], BF16, name=f"h_bf1{s}", align_bytes=64) for s in range(2)}
-        for s in range(2):
-            h_bf[0, s] = stage.tile([P, HALF, PACK], BF16, name=f"h_bf0{s}", offset=w1_at[s, 1], align_bytes=64)
-        banks = [psum.tile([P, HALF], F32, name=f"bank{i}") for i in range(8)]
+        bounded[1, 0] = stage.tile([P, PACK, HALF], F32, name="bounded10", offset=4 * SLOT)
+        shares = {(0, 0): 128, (0, 1): 128, (1, 0): 128, (1, 1): 128}
+        h_at = {(0, 0): SLOT, (0, 1): SLOT - 2048, (1, 0): SLOT - 2048, (1, 1): 6 * SLOT}
+        h_bf = {k: stage.tile([P, HALF, PACK], BF16, name="h_bf%d%d" % k, offset=v, align_bytes=64) for k, v in h_at.items()}
+        banks = [psum.tile([P, HALF], F32, name=f"bank{i}") for i in range(7)]
+
+        def bank_of(stage_no, s, i):
+            return (8 * stage_no + 4 * s + i) % 7
+
         results = [keep.tile([P, HALF], F32, name=f"result{i}") for i in range(8)]
 
         def load_table_scales():
@@ -127,36 +137,40 @@ def tile_list_aligned_error_gate_kernel(tc, tab_words, tab_scales, offs, w1, g, 
 
         def w1_pass(a, b, s, t):
             cols = slice(P * t, P * (t + 1))
-            table_pass(4 * s + t, w1_codes[a, b][:, cols], w1_sc[a, b][:, cols], a, s)
+            table_pass(bank_of(b, s, t), w1_codes[a, b][:, cols], w1_sc[a, b][:, cols], a, s)
 
         def bound(b, s, t):
-            nc.scalar.activation(out=bounded[b, s][:, t, :], in_=banks[4 * s + t][:], func=ACT.Tanh)
+            nc.scalar.activation(out=bounded[b, s][:, t, :], in_=banks[bank_of(b, s, t)][:], func=ACT.Tanh)
 
         def direct(s, n):
             cols = slice(P * n, P * (n + 1))
             for a in range(2):
-                table_pass(4 * s + n, wd_codes[:, a, cols], wd_sc[:, a, :].bitcast(U8)[:, cols], a, s)
+                table_pass(bank_of(2, s, n), wd_codes[:, a, cols], wd_sc[:, a, :].bitcast(U8)[:, cols], a, s)
 
         def make_gate(s, n):
-            nc.scalar.activation(out=gate[:, n, HALF * s : HALF * (s + 1)], in_=banks[4 * s + n][:], func=ACT.Sigmoid)
+            nc.scalar.activation(out=gate[:, n, HALF * s : HALF * (s + 1)], in_=banks[bank_of(2, s, n)][:], func=ACT.Sigmoid)
 
-        def apply_gain(b, s):
-            nc.vector.tensor_tensor(
-                out=h_bf[b, s][:].rearrange("p (c i) t -> p c t i", i=4),
-                in0=bounded[b, s][:].rearrange("p t (c i) -> p c t i", i=4),
-                in1=gain[:, b, :].unsqueeze(1).unsqueeze(3).to_broadcast([P, HALF // 4, PACK, 4]),
+        def gain_part(engine, factors, b, s, c0, c1):
+            engine.tensor_tensor(
+                out=h_bf[b, s][:, c0:c1, :].rearrange("p (c i) t -> p c t i", i=4),
+                in0=bounded[b, s][:, :, c0:c1].rearrange("p t (c i) -> p c t i", i=4),
+                in1=factors[:, b, :].unsqueeze(1).unsqueeze(3).to_broadcast([P, (c1 - c0) // 4, PACK, 4]),
                 op=MULT,
             )
 
+        def apply_gain(b, s):
+            gain_part(nc.gpsimd, gain, b, s, HALF - shares[b, s], HALF)
+            gain_part(nc.vector, gain_ps, b, s, 0, HALF - shares[b, s])
+
         def quantize_h(b, s):
             cols = slice(HALF * s, HALF * (s + 1))
-            nc.vector.quantize_mx(out=h_codes[b][:, cols].bitcast(E4M3), scales=h_sc[b][:, cols], in_=h_bf[b, s][:].rearrange("p c t -> p (c t)"))
+            nc.vector.quantize_mx(out=h_codes[b, s][:].bitcast(E4M3), scales=h_sc[b][:, cols], in_=h_bf[b, s][:].rearrange("p c t -> p (c t)"))
 
         def w2_pass(b, s, n, bank):
             cols = slice(HALF * s, HALF * (s + 1))
             rows = slice(N * b + P * n, N * b + P * (n + 1))
             nc.tensor.matmul_mx(out=banks[bank][:], lhsT=w2_codes[:, rows].bitcast(E4M3), lhsT_scale=w2_sc[:, rows],
-                                rhs=h_codes[b][:, cols].bitcast(E4M3), rhs_scale=h_sc[b][:, cols],
+                                rhs=h_codes[b, s][:].bitcast(E4M3), rhs_scale=h_sc[b][:, cols],
                                 start=(b == 0), stop=(b == 1))
 
         def finish(s, n, bank):
@@ -173,7 +187,12 @@ def tile_list_aligned_error_gate_kernel(tc, tab_words, tab_scales, offs, w1, g, 
         nc.scalar.activation(out=warm_out[:], in_=warm_in[:], func=ACT.Sigmoid)
         nc.gpsimd.memset(moved_sc[0][:], 0)
         nc.gpsimd.memset(moved_sc[1][:], 0)
-        nc.gpsimd.dma_start(out=gain[:], in_=g.rearrange("(b p t) -> p b t", b=2, t=PACK))
+        nc.gpsimd.memset(gain_rows[:], 0.0)
+        nc.gpsimd.dma_start(out=gain_rows[0:2, :], in_=g.rearrange("(b r) -> b r", b=2))
+        make_identity(nc, ident[:])
+        for t in range(PACK):
+            nc.tensor.transpose(gain_ps[:, :, t], gain_rows[:].rearrange("b (p t) -> b p t", t=PACK)[:, :, t], ident[:])
+        nc.scalar.copy(gain[:], gain_ps[:, 0:2, :])
         load_table(0)
         load_w1(0, 0)
         load_table(1)
@@ -190,7 +209,8 @@ def tile_list_aligned_error_gate_kernel(tc, tab_words, tab_scales, offs, w1, g, 
         quantize_w1(0, 0)
         for s in range(2):
             for t in range(PACK):
-                w1_pass(0, 0, s, t)
+                if (s, t) != (1, 3):
+                    w1_pass(0, 0, s, t)
         gather_codes(1, 0)
         gather_codes(1, 1)
         load_w2(1)
@@ -204,41 +224,48 @@ def tile_list_aligned_error_gate_kernel(tc, tab_words, tab_scales, offs, w1, g, 
         quantize_pair(1)
         for s in range(2):
             for t in range(PACK):
+                if (s, t) == (1, 3):
+                    w1_pass(0, 0, s, t)
                 w1_pass(1, 0, s, t)
                 bound(0, s, t)
         cast_w1("vector", 0, 1, 0, 128)
         quantize_w1(0, 1)
         apply_gain(0, 0)
-        cast_w1("vector", 1, 1, 0, 128)
+        cast_w1("vector", 1, 1, 0, 92)
+        cast_w1("scalar", 1, 1, 92, 128)
         quantize_h(0, 0)
         quantize_w1(1, 1)
         cast_w2("scalar", 0, 0, 512)
         for s in range(2):
             for t in range(PACK):
                 w1_pass(0, 1, s, t)
-            for t in range(PACK):
                 w1_pass(1, 1, s, t)
                 bound(1, s, t)
         apply_gain(0, 1)
-        quantize_w2(0)
+        cast_w2("vector", 1, 0, 512)
         quantize_h(0, 1)
-        cast_w2("scalar", 1, 0, 512)
+        quantize_w2(0)
         for s in range(2):
             for n in range(4):
-                direct(s, n)
+                if (s, n) != (1, 3):
+                    direct(s, n)
         apply_gain(1, 0)
-        apply_gain(1, 1)
-        quantize_h(1, 0)
         quantize_w2(1)
+        quantize_h(1, 0)
+        make_gate(0, 0)
+        direct(1, 3)
         for n in range(4):
-            make_gate(0, n)
-            w2_pass(0, 0, n, n)
-            w2_pass(1, 0, n, n)
-        quantize_h(1, 1)
-        for n in range(4):
-            finish(0, n, n)
-        for n in range(4):
+            make_gate((n + 1) // 4, (n + 1) % 4)
+            w2_pass(0, 0, n, bank_of(3, 0, n))
+            w2_pass(1, 0, n, bank_of(3, 0, n))
+        for n in range(1, 4):
             make_gate(1, n)
-            w2_pass(0, 1, n, n)
-            w2_pass(1, 1, n, n)
-            finish(1, n, n)
+        apply_gain(1, 1)
+        finish(0, 0, bank_of(3, 0, 0))
+        quantize_h(1, 1)
+        for n in range(1, 4):
+            finish(0, n, bank_of(3, 0, n))
+        for n in range(4):
+            w2_pass(0, 1, n, bank_of(3, 1, n))
+            w2_pass(1, 1, n, bank_of(3, 1, n))
+            finish(1, n, bank_of(3, 1, n))

@@ -44,23 +44,24 @@ def tile_list_aligned_error_gate_kernel(tc, tab_words, tab_scales, offs, w1, g, 
         gain_ps = psum.tile([P, P, PACK], F32, name="gain_ps")
         w1_at = {(0, 0): 4 * SLOT, (1, 0): scales_at + T - 64, (0, 1): SLOT, (1, 1): 0}
         w1_raw = {k: stage.tile([P, PACK, PASS], F32, name="w1_raw%d%d" % k, offset=v) for k, v in w1_at.items()}
-        w2_raw = [stage.tile([P, PACK, N], F32, name=f"w2_raw{b}", offset=(4 + b) * SLOT) for b in range(2)]
-        wd_codes = stage.tile([P, 2, N], I32, name="wd_codes", offset=w1_at[1, 0], align_bytes=64)
+        w2_raw = [stage.tile([P, PACK, N], F32, name=f"w2_raw{b}", offset=(4 * SLOT, w1_at[1, 0])[b]) for b in range(2)]
+        wd_codes = stage.tile([P, 2, N], I32, name="wd_codes", offset=5 * SLOT, align_bytes=64)
         v_codes = [keep.tile([P, S], U32, name=f"v_codes{a}", align_bytes=64) for a in range(2)]
         picked_sc = keep.tile([P, S], U8, name="picked_sc", align_bytes=64)
         moved_sc = [keep.tile([P, S // 4], I32, name=f"moved_sc{a}", align_bytes=64) for a in range(2)]
         v_sc = [moved_sc[a][:].bitcast(U8) for a in range(2)]
-        wd_sc = stage.tile([P, 2, N // 4], I32, name="wd_sc", offset=w1_at[1, 0] + 4096, align_bytes=64)
-        w1_bf = {(a, b): keep.tile([P, PACK, P, PACK], BF16, name=f"w1_bf{a}{b}", align_bytes=64) for a, b in ((0, 0), (0, 1), (1, 1))}
+        wd_sc = stage.tile([P, 2, N // 4], I32, name="wd_sc", offset=7 * SLOT, align_bytes=64)
+        w1_bf = {(a, b): keep.tile([P, PACK, P, PACK], BF16, name=f"w1_bf{a}{b}", align_bytes=64) for a, b in ((0, 1), (1, 1))}
+        w1_bf[0, 0] = stage.tile([P, PACK, P, PACK], BF16, name="w1_bf00", offset=7 * SLOT, align_bytes=64)
         w1_pair = [keep.tile([P, 2, P, PACK], BF16, name=f"w1_pair{u}", align_bytes=64) for u in range(2)]
-        w2_bf = [keep.tile([P, N * PACK], BF16, name="w2_bf0", align_bytes=64),
+        w2_bf = [stage.tile([P, N * PACK], BF16, name="w2_bf0", offset=8 * SLOT, align_bytes=64),
                  stage.tile([P, N * PACK], BF16, name="w2_bf1", offset=6 * SLOT, align_bytes=64)]
         w1_codes = {(a, b): keep.tile([P, PASS], U32, name=f"w1_codes{a}{b}", align_bytes=64) for a in range(2) for b in range(2)}
         w1_sc = {(a, b): keep.tile([P, PASS], U8, name=f"w1_sc{a}{b}", align_bytes=64) for a in range(2) for b in range(2)}
-        w2_codes = keep.tile([P, 2 * N], U32, name="w2_codes", align_bytes=64)
+        w2_codes = [stage.tile([P, N], U32, name=f"w2_codes{b}", offset=(w1_at[1, 0] + 2048, 8 * SLOT)[b], align_bytes=64) for b in range(2)]
         w2_sc = keep.tile([P, 2 * N], U8, name="w2_sc", align_bytes=64)
         h_codes = {(b, s): keep.tile([P, HALF], U32, name=f"h_codes{b}{s}", align_bytes=64) for b, s in ((0, 0), (1, 0), (1, 1))}
-        h_codes[0, 1] = stage.tile([P, HALF], U32, name="h_codes01", offset=5 * SLOT, align_bytes=64)
+        h_codes[0, 1] = stage.tile([P, HALF], U32, name="h_codes01", offset=w1_at[1, 0], align_bytes=64)
         h_sc = [stage.tile([P, S], U8, name="h_sc0", offset=w1_at[1, 1], align_bytes=64), keep.tile([P, S], U8, name="h_sc1", align_bytes=64)]
         gate = keep.tile([P, N // P, S], F32, name="gate")
         bounded = {(b, s): keep.tile([P, PACK, HALF], F32, name=f"bounded{b}{s}") for b, s in ((0, 0), (0, 1), (1, 1))}
@@ -127,17 +128,17 @@ def tile_list_aligned_error_gate_kernel(tc, tab_words, tab_scales, offs, w1, g, 
 
         def quantize_w2(b):
             cols = slice(N * b, N * (b + 1))
-            nc.vector.quantize_mx(out=w2_codes[:, cols].bitcast(E4M3), scales=w2_sc[:, cols], in_=w2_bf[b][:])
+            nc.vector.quantize_mx(out=w2_codes[b][:].bitcast(E4M3), scales=w2_sc[:, cols], in_=w2_bf[b][:])
 
-        def table_pass(bank, codes, scales, a, s):
+        def table_pass(bank, codes, scales, a, s, first):
             cols = slice(HALF * s, HALF * (s + 1))
             nc.tensor.matmul_mx(out=banks[bank][:], lhsT=codes.bitcast(E4M3), lhsT_scale=scales,
                                 rhs=v_codes[a][:, cols].bitcast(E5M2), rhs_scale=v_sc[a][:, cols],
-                                start=(a == 0), stop=(a == 1))
+                                start=first, stop=not first)
 
-        def w1_pass(a, b, s, t):
+        def w1_pass(a, b, s, t, first):
             cols = slice(P * t, P * (t + 1))
-            table_pass(bank_of(b, s, t), w1_codes[a, b][:, cols], w1_sc[a, b][:, cols], a, s)
+            table_pass(bank_of(b, s, t), w1_codes[a, b][:, cols], w1_sc[a, b][:, cols], a, s, first)
 
         def bound(b, s, t):
             nc.scalar.activation(out=bounded[b, s][:, t, :], in_=banks[bank_of(b, s, t)][:], func=ACT.Tanh)
@@ -145,7 +146,7 @@ def tile_list_aligned_error_gate_kernel(tc, tab_words, tab_scales, offs, w1, g, 
         def direct(s, n):
             cols = slice(P * n, P * (n + 1))
             for a in range(2):
-                table_pass(bank_of(2, s, n), wd_codes[:, a, cols], wd_sc[:, a, :].bitcast(U8)[:, cols], a, s)
+                table_pass(bank_of(2, s, n), wd_codes[:, a, cols], wd_sc[:, a, :].bitcast(U8)[:, cols], a, s, a == 0)
 
         def make_gate(s, n):
             nc.scalar.activation(out=gate[:, n, HALF * s : HALF * (s + 1)], in_=banks[bank_of(2, s, n)][:], func=ACT.Sigmoid)
@@ -166,12 +167,12 @@ def tile_list_aligned_error_gate_kernel(tc, tab_words, tab_scales, offs, w1, g, 
             cols = slice(HALF * s, HALF * (s + 1))
             nc.vector.quantize_mx(out=h_codes[b, s][:].bitcast(E4M3), scales=h_sc[b][:, cols], in_=h_bf[b, s][:].rearrange("p c t -> p (c t)"))
 
-        def w2_pass(b, s, n, bank):
+        def w2_pass(b, s, n, bank, first):
             cols = slice(HALF * s, HALF * (s + 1))
             rows = slice(N * b + P * n, N * b + P * (n + 1))
-            nc.tensor.matmul_mx(out=banks[bank][:], lhsT=w2_codes[:, rows].bitcast(E4M3), lhsT_scale=w2_sc[:, rows],
+            nc.tensor.matmul_mx(out=banks[bank][:], lhsT=w2_codes[b][:, P * n : P * (n + 1)].bitcast(E4M3), lhsT_scale=w2_sc[:, rows],
                                 rhs=h_codes[b, s][:].bitcast(E4M3), rhs_scale=h_sc[b][:, cols],
-                                start=(b == 0), stop=(b == 1))
+                                start=first, stop=not first)
 
         def finish(s, n, bank):
             cols = slice(HALF * s, HALF * (s + 1))
@@ -207,26 +208,25 @@ def tile_list_aligned_error_gate_kernel(tc, tab_words, tab_scales, offs, w1, g, 
         cast_w1("vector", 0, 0, 64, 128)
         load_w2(0)
         quantize_w1(0, 0)
-        for s in range(2):
-            for t in range(PACK):
-                if (s, t) != (1, 3):
-                    w1_pass(0, 0, s, t)
+        early = [(0, t) for t in range(PACK)] + [(1, 0)]
+        for s, t in early:
+            w1_pass(0, 0, s, t, True)
         gather_codes(1, 0)
         gather_codes(1, 1)
-        load_w2(1)
-        cast_pair("vector", 0)
-        cast_pair("scalar", 1)
         nc.gpsimd.memset(wd_sc[:], 0)
         nc.sync.dma_start(out=wd_codes[:], in_=wd_words.rearrange("a p c i -> p a (c i)").bitcast(I32))
         for q in range(4):
             nc.sync.dma_start(out=wd_sc[32 * q : 32 * q + 4, :, :], in_=wd_scales[:, 4 * q : 4 * q + 4, :].rearrange("a r c -> r a c").bitcast(I32))
+        cast_pair("vector", 0)
+        cast_pair("scalar", 1)
+        load_w2(1)
         quantize_pair(0)
         quantize_pair(1)
         for s in range(2):
             for t in range(PACK):
-                if (s, t) == (1, 3):
-                    w1_pass(0, 0, s, t)
-                w1_pass(1, 0, s, t)
+                w1_pass(1, 0, s, t, (s, t) not in early)
+                if (s, t) not in early:
+                    w1_pass(0, 0, s, t, False)
                 bound(0, s, t)
         cast_w1("vector", 0, 1, 0, 128)
         quantize_w1(0, 1)
@@ -238,8 +238,8 @@ def tile_list_aligned_error_gate_kernel(tc, tab_words, tab_scales, offs, w1, g, 
         cast_w2("scalar", 0, 0, 512)
         for s in range(2):
             for t in range(PACK):
-                w1_pass(0, 1, s, t)
-                w1_pass(1, 1, s, t)
+                w1_pass(0, 1, s, t, True)
+                w1_pass(1, 1, s, t, False)
                 bound(1, s, t)
         apply_gain(0, 1)
         cast_w2("vector", 1, 0, 512)
@@ -256,8 +256,8 @@ def tile_list_aligned_error_gate_kernel(tc, tab_words, tab_scales, offs, w1, g, 
         direct(1, 3)
         for n in range(4):
             make_gate((n + 1) // 4, (n + 1) % 4)
-            w2_pass(0, 0, n, bank_of(3, 0, n))
-            w2_pass(1, 0, n, bank_of(3, 0, n))
+            w2_pass(n // 2, 0, n, bank_of(3, 0, n), True)
+            w2_pass(1 - n // 2, 0, n, bank_of(3, 0, n), False)
         for n in range(1, 4):
             make_gate(1, n)
         apply_gain(1, 1)
@@ -266,6 +266,6 @@ def tile_list_aligned_error_gate_kernel(tc, tab_words, tab_scales, offs, w1, g, 
         for n in range(1, 4):
             finish(0, n, bank_of(3, 0, n))
         for n in range(4):
-            w2_pass(0, 1, n, bank_of(3, 1, n))
-            w2_pass(1, 1, n, bank_of(3, 1, n))
+            w2_pass(1, 1, n, bank_of(3, 1, n), True)
+            w2_pass(0, 1, n, bank_of(3, 1, n), False)
             finish(1, n, bank_of(3, 1, n))

@@ -16,13 +16,17 @@ E4M3 = mybir.dt.float8_e4m3fn_x4
 E5M2 = mybir.dt.float8_e5m2_x4
 ACT = mybir.ActivationFunctionType
 MULT = mybir.AluOpType.mult
-ADD = mybir.AluOpType.add
 
 P = 128
 PACK = 4
 PASS = P * PACK
-HALF = 512
+HALF = S // 2
 SLOT = 8192
+EDGE = 64
+BANKS = 7
+GPSIMD_COLUMNS = 128
+VECTOR_GROUPS = 92
+EARLY = [(0, 0), (0, 1), (0, 2), (0, 3), (1, 0)]
 
 
 def tile_list_aligned_error_gate_kernel(tc, tab_words, tab_scales, offs, w1, g, w2, wd_words, wd_scales, out):
@@ -33,51 +37,50 @@ def tile_list_aligned_error_gate_kernel(tc, tab_words, tab_scales, offs, w1, g, 
         psum = ctx.enter_context(tc.psum_pool(name="psum", bufs=1))
 
         offsets = keep.tile([P, S // 16], U16, name="offsets")
-        scales_at = 2 * SLOT - 64
         warm_in = keep.tile([P, 16], F32, name="warm_in")
         warm_out = keep.tile([P, 16], F32, name="warm_out")
-        table = [stage.tile([P, T], I32, name=f"table{a}", offset=(0, 5 * SLOT)[a], align_bytes=64) for a in range(2)]
+        table_at = (0, 5 * SLOT)
+        table = [stage.tile([P, T], I32, name=f"table{a}", offset=table_at[a], align_bytes=64) for a in range(2)]
+        scales_at = 2 * SLOT - EDGE
         table_sc = stage.tile([P, T // 4], I32, name="table_sc", offset=scales_at, align_bytes=64)
         gain = keep.tile([P, 2, PACK], F32, name="gain")
         gain_rows = keep.tile([P, PASS], F32, name="gain_rows")
         ident = keep.tile([P, P], F32, name="ident")
         gain_ps = psum.tile([P, P, PACK], F32, name="gain_ps")
-        w1_at = {(0, 0): 4 * SLOT, (1, 0): scales_at + T - 64, (0, 1): SLOT, (1, 1): 0}
+
+        w1_at = {(0, 0): 4 * SLOT, (1, 0): scales_at + T - EDGE, (0, 1): SLOT, (1, 1): 0}
         w1_raw = {k: stage.tile([P, PACK, PASS], F32, name="w1_raw%d%d" % k, offset=v) for k, v in w1_at.items()}
-        w2_raw = [stage.tile([P, PACK, N], F32, name=f"w2_raw{b}", offset=(4 * SLOT, w1_at[1, 0])[b]) for b in range(2)]
-        wd_codes = stage.tile([P, 2, N], I32, name="wd_codes", offset=5 * SLOT, align_bytes=64)
+        w2_raw = [stage.tile([P, PACK, N], F32, name=f"w2_raw{b}", offset=(w1_at[0, 0], table_at[1])[b]) for b in range(2)]
+        wd_codes = stage.tile([P, 2, N], I32, name="wd_codes", offset=w1_at[1, 0], align_bytes=64)
         v_codes = [keep.tile([P, S], U32, name=f"v_codes{a}", align_bytes=64) for a in range(2)]
         picked_sc = keep.tile([P, S], U8, name="picked_sc", align_bytes=64)
         moved_sc = [keep.tile([P, S // 4], I32, name=f"moved_sc{a}", align_bytes=64) for a in range(2)]
         v_sc = [moved_sc[a][:].bitcast(U8) for a in range(2)]
-        wd_sc = stage.tile([P, 2, N // 4], I32, name="wd_sc", offset=7 * SLOT, align_bytes=64)
-        w1_bf = {(a, b): keep.tile([P, PACK, P, PACK], BF16, name=f"w1_bf{a}{b}", align_bytes=64) for a, b in ((0, 1), (1, 1))}
-        w1_bf[0, 0] = stage.tile([P, PACK, P, PACK], BF16, name="w1_bf00", offset=7 * SLOT, align_bytes=64)
+
+        wd_sc = stage.tile([P, 2, N // 4], I32, name="wd_sc", offset=w1_at[1, 0] + 8 * N, align_bytes=64)
+        bf_at = {(0, 0): 7 * SLOT, (0, 1): 10 * SLOT, (1, 1): 9 * SLOT}
+        w1_bf = {k: stage.tile([P, PACK, P, PACK], BF16, name="w1_bf%d%d" % k, offset=v, align_bytes=64) for k, v in bf_at.items()}
+        gain_late = stage.tile([P, 2, PACK], F32, name="gain_late", offset=bf_at[0, 1])
         w1_pair = [keep.tile([P, 2, P, PACK], BF16, name=f"w1_pair{u}", align_bytes=64) for u in range(2)]
-        w2_bf = [stage.tile([P, N * PACK], BF16, name="w2_bf0", offset=8 * SLOT, align_bytes=64),
-                 stage.tile([P, N * PACK], BF16, name="w2_bf1", offset=6 * SLOT, align_bytes=64)]
+        w2_bf_at = (8 * SLOT, 6 * SLOT)
+        w2_bf = [stage.tile([P, N * PACK], BF16, name=f"w2_bf{b}", offset=w2_bf_at[b], align_bytes=64) for b in range(2)]
         w1_codes = {(a, b): keep.tile([P, PASS], U32, name=f"w1_codes{a}{b}", align_bytes=64) for a in range(2) for b in range(2)}
         w1_sc = {(a, b): keep.tile([P, PASS], U8, name=f"w1_sc{a}{b}", align_bytes=64) for a in range(2) for b in range(2)}
-        w2_codes = [stage.tile([P, N], U32, name=f"w2_codes{b}", offset=(w1_at[1, 0] + 2048, 8 * SLOT)[b], align_bytes=64) for b in range(2)]
+        w2_codes = [stage.tile([P, N], U32, name=f"w2_codes{b}", offset=(table_at[1] + 4 * HALF, w2_bf_at[0])[b], align_bytes=64) for b in range(2)]
         w2_sc = keep.tile([P, 2 * N], U8, name="w2_sc", align_bytes=64)
         h_codes = {(b, s): keep.tile([P, HALF], U32, name=f"h_codes{b}{s}", align_bytes=64) for b, s in ((0, 0), (1, 0), (1, 1))}
-        h_codes[0, 1] = stage.tile([P, HALF], U32, name="h_codes01", offset=w1_at[1, 0], align_bytes=64)
+        h_codes[0, 1] = stage.tile([P, HALF], U32, name="h_codes01", offset=table_at[1], align_bytes=64)
         h_sc = [stage.tile([P, S], U8, name="h_sc0", offset=w1_at[1, 1], align_bytes=64), keep.tile([P, S], U8, name="h_sc1", align_bytes=64)]
         gate = keep.tile([P, N // P, S], F32, name="gate")
         bounded = {(b, s): keep.tile([P, PACK, HALF], F32, name=f"bounded{b}{s}") for b, s in ((0, 0), (0, 1), (1, 1))}
-        bounded[1, 0] = stage.tile([P, PACK, HALF], F32, name="bounded10", offset=4 * SLOT)
-        shares = {(0, 0): 128, (0, 1): 128, (1, 0): 128, (1, 1): 128}
-        h_at = {(0, 0): SLOT, (0, 1): SLOT - 2048, (1, 0): SLOT - 2048, (1, 1): 6 * SLOT}
+        bounded[1, 0] = stage.tile([P, PACK, HALF], F32, name="bounded10", offset=w1_at[0, 0])
+        h_at = {(0, 0): w1_at[0, 1], (0, 1): bf_at[1, 1], (1, 0): bf_at[1, 1], (1, 1): w2_bf_at[1]}
         h_bf = {k: stage.tile([P, HALF, PACK], BF16, name="h_bf%d%d" % k, offset=v, align_bytes=64) for k, v in h_at.items()}
-        banks = [psum.tile([P, HALF], F32, name=f"bank{i}") for i in range(7)]
-
-        def bank_of(stage_no, s, i):
-            return (8 * stage_no + 4 * s + i) % 7
-
+        banks = [psum.tile([P, HALF], F32, name=f"bank{i}") for i in range(BANKS)]
         results = [keep.tile([P, HALF], F32, name=f"result{i}") for i in range(8)]
 
-        def load_table_scales():
-            nc.sync.dma_start(out=table_sc[0:32, :], in_=tab_scales.rearrange("a q t -> (a q) t").bitcast(I32))
+        def bank_of(kind, s, i):
+            return banks[(8 * kind + 4 * s + i) % BANKS]
 
         def load_table(a):
             nc.sync.dma_start(out=table[a][:], in_=tab_words[a].rearrange("p t i -> p (t i)").bitcast(I32))
@@ -94,30 +97,26 @@ def tile_list_aligned_error_gate_kernel(tc, tab_words, tab_scales, offs, w1, g, 
             for q in range(4):
                 nc.sync.dma_start(out=moved_sc[a][32 * q : 32 * q + 4, :], in_=picked_sc[16 * a + 4 * q : 16 * a + 4 * q + 4, :].bitcast(I32))
 
-        def gather_codes(a, s):
-            window = table[a][:].bitcast(U32).indirect(offsets[:, 32 * s : 32 * (s + 1)])
-            nc.vector.tensor_copy(v_codes[a][:, HALF * s : HALF * (s + 1)], window)
-
-        def cast(engine, dst, src):
+        def round_on(engine, dst, src):
             if engine == "vector":
                 nc.vector.tensor_copy(out=dst, in_=src)
             else:
                 nc.scalar.activation(out=dst, in_=src, func=ACT.Copy)
 
-        def cast_w1(engine, a, b, m0, m1):
+        def round_w1(engine, a, b, m0, m1):
             dst = w1_bf[a, b][:, :, m0:m1, :].rearrange("p t m j -> p m j t")
             src = w1_raw[a, b][:, :, PACK * m0 : PACK * m1].rearrange("p j (m t) -> p m j t", t=PACK)
-            cast(engine, dst, src)
+            round_on(engine, dst, src)
 
-        def cast_pair(engine, u):
+        def round_pair(engine, u):
             dst = w1_pair[u][:].rearrange("p t m j -> p m j t")
             src = w1_raw[1, 0][:].rearrange("p j (m t) -> p m j t", t=PACK)[:, :, :, 2 * u : 2 * u + 2]
-            cast(engine, dst, src)
+            round_on(engine, dst, src)
 
-        def cast_w2(engine, b, c0, c1):
-            dst = w2_bf[b][:, PACK * c0 : PACK * c1].rearrange("p (c i j) -> p c j i", i=4, j=PACK)
-            src = w2_raw[b][:, :, c0:c1].rearrange("p j (c i) -> p c j i", i=4)
-            cast(engine, dst, src)
+        def round_w2(engine, b):
+            dst = w2_bf[b][:].rearrange("p (c i j) -> p c j i", i=4, j=PACK)
+            src = w2_raw[b][:].rearrange("p j (c i) -> p c j i", i=4)
+            round_on(engine, dst, src)
 
         def quantize_w1(a, b):
             nc.vector.quantize_mx(out=w1_codes[a, b][:].bitcast(E4M3), scales=w1_sc[a, b][:], in_=w1_bf[a, b][:].rearrange("p t m j -> p (t m j)"))
@@ -127,12 +126,15 @@ def tile_list_aligned_error_gate_kernel(tc, tab_words, tab_scales, offs, w1, g, 
             nc.vector.quantize_mx(out=w1_codes[1, 0][:, cols].bitcast(E4M3), scales=w1_sc[1, 0][:, cols], in_=w1_pair[u][:].rearrange("p t m j -> p (t m j)"))
 
         def quantize_w2(b):
-            cols = slice(N * b, N * (b + 1))
-            nc.vector.quantize_mx(out=w2_codes[b][:].bitcast(E4M3), scales=w2_sc[:, cols], in_=w2_bf[b][:])
+            nc.vector.quantize_mx(out=w2_codes[b][:].bitcast(E4M3), scales=w2_sc[:, N * b : N * (b + 1)], in_=w2_bf[b][:])
+
+        def quantize_h(b, s):
+            nc.vector.quantize_mx(out=h_codes[b, s][:].bitcast(E4M3), scales=h_sc[b][:, HALF * s : HALF * (s + 1)],
+                                  in_=h_bf[b, s][:].rearrange("p c t -> p (c t)"))
 
         def table_pass(bank, codes, scales, a, s, first):
             cols = slice(HALF * s, HALF * (s + 1))
-            nc.tensor.matmul_mx(out=banks[bank][:], lhsT=codes.bitcast(E4M3), lhsT_scale=scales,
+            nc.tensor.matmul_mx(out=bank[:], lhsT=codes.bitcast(E4M3), lhsT_scale=scales,
                                 rhs=v_codes[a][:, cols].bitcast(E5M2), rhs_scale=v_sc[a][:, cols],
                                 start=first, stop=not first)
 
@@ -140,16 +142,23 @@ def tile_list_aligned_error_gate_kernel(tc, tab_words, tab_scales, offs, w1, g, 
             cols = slice(P * t, P * (t + 1))
             table_pass(bank_of(b, s, t), w1_codes[a, b][:, cols], w1_sc[a, b][:, cols], a, s, first)
 
-        def bound(b, s, t):
-            nc.scalar.activation(out=bounded[b, s][:, t, :], in_=banks[bank_of(b, s, t)][:], func=ACT.Tanh)
-
-        def direct(s, n):
+        def direct_product(s, n):
             cols = slice(P * n, P * (n + 1))
             for a in range(2):
                 table_pass(bank_of(2, s, n), wd_codes[:, a, cols], wd_sc[:, a, :].bitcast(U8)[:, cols], a, s, a == 0)
 
+        def w2_product(s, n, opening):
+            for b in (opening, 1 - opening):
+                nc.tensor.matmul_mx(out=bank_of(3, s, n)[:], lhsT=w2_codes[b][:, P * n : P * (n + 1)].bitcast(E4M3),
+                                    lhsT_scale=w2_sc[:, N * b + P * n : N * b + P * (n + 1)],
+                                    rhs=h_codes[b, s][:].bitcast(E4M3), rhs_scale=h_sc[b][:, HALF * s : HALF * (s + 1)],
+                                    start=(b == opening), stop=(b != opening))
+
+        def bound(b, s, t):
+            nc.scalar.activation(out=bounded[b, s][:, t, :], in_=bank_of(b, s, t)[:], func=ACT.Tanh)
+
         def make_gate(s, n):
-            nc.scalar.activation(out=gate[:, n, HALF * s : HALF * (s + 1)], in_=banks[bank_of(2, s, n)][:], func=ACT.Sigmoid)
+            nc.scalar.activation(out=gate[:, n, HALF * s : HALF * (s + 1)], in_=bank_of(2, s, n)[:], func=ACT.Sigmoid)
 
         def gain_part(engine, factors, b, s, c0, c1):
             engine.tensor_tensor(
@@ -160,40 +169,31 @@ def tile_list_aligned_error_gate_kernel(tc, tab_words, tab_scales, offs, w1, g, 
             )
 
         def apply_gain(b, s):
-            gain_part(nc.gpsimd, gain, b, s, HALF - shares[b, s], HALF)
-            gain_part(nc.vector, gain_ps, b, s, 0, HALF - shares[b, s])
+            gain_part(nc.gpsimd, gain_late, b, s, HALF - GPSIMD_COLUMNS, HALF)
+            gain_part(nc.vector, gain_ps, b, s, 0, HALF - GPSIMD_COLUMNS)
 
-        def quantize_h(b, s):
-            cols = slice(HALF * s, HALF * (s + 1))
-            nc.vector.quantize_mx(out=h_codes[b, s][:].bitcast(E4M3), scales=h_sc[b][:, cols], in_=h_bf[b, s][:].rearrange("p c t -> p (c t)"))
-
-        def w2_pass(b, s, n, bank, first):
-            cols = slice(HALF * s, HALF * (s + 1))
-            rows = slice(N * b + P * n, N * b + P * (n + 1))
-            nc.tensor.matmul_mx(out=banks[bank][:], lhsT=w2_codes[b][:, P * n : P * (n + 1)].bitcast(E4M3), lhsT_scale=w2_sc[:, rows],
-                                rhs=h_codes[b, s][:].bitcast(E4M3), rhs_scale=h_sc[b][:, cols],
-                                start=first, stop=not first)
-
-        def finish(s, n, bank):
+        def finish(s, n):
             cols = slice(HALF * s, HALF * (s + 1))
             result = results[4 * s + n]
-            nc.vector.tensor_tensor(out=result[:], in0=banks[bank][:], in1=gate[:, n, cols], op=MULT)
+            nc.vector.tensor_tensor(out=result[:], in0=bank_of(3, s, n)[:], in1=gate[:, n, cols], op=MULT)
             nc.sync.dma_start(out=out[P * n : P * (n + 1), cols], in_=result[:])
 
         nc.sync.dma_start(offsets[:], offs)
-        load_table_scales()
+        nc.sync.dma_start(out=table_sc[0:32, :], in_=tab_scales.rearrange("a q t -> (a q) t").bitcast(I32))
         nc.gpsimd.memset(warm_in[:], 0.0)
         nc.gpsimd.memset(table_sc[32:64, :], 0)
         nc.vector.memset(table_sc[64:128, :], 0)
         nc.scalar.activation(out=warm_out[:], in_=warm_in[:], func=ACT.Sigmoid)
         nc.gpsimd.memset(moved_sc[0][:], 0)
         nc.gpsimd.memset(moved_sc[1][:], 0)
+
         nc.gpsimd.memset(gain_rows[:], 0.0)
         nc.gpsimd.dma_start(out=gain_rows[0:2, :], in_=g.rearrange("(b r) -> b r", b=2))
         make_identity(nc, ident[:])
         for t in range(PACK):
             nc.tensor.transpose(gain_ps[:, :, t], gain_rows[:].rearrange("b (p t) -> b p t", t=PACK)[:, :, t], ident[:])
         nc.scalar.copy(gain[:], gain_ps[:, 0:2, :])
+
         load_table(0)
         load_w1(0, 0)
         load_table(1)
@@ -204,68 +204,68 @@ def tile_list_aligned_error_gate_kernel(tc, tab_words, tab_scales, offs, w1, g, 
         load_w1(0, 1)
         nc.vector.tensor_copy(v_codes[0][:], table[0][:].bitcast(U32).indirect(offsets[:]))
         load_w1(1, 1)
-        cast_w1("scalar", 0, 0, 0, 64)
-        cast_w1("vector", 0, 0, 64, 128)
+        round_w1("scalar", 0, 0, 0, P // 2)
+        round_w1("vector", 0, 0, P // 2, P)
         load_w2(0)
         quantize_w1(0, 0)
-        early = [(0, t) for t in range(PACK)] + [(1, 0)]
-        for s, t in early:
+        for s, t in EARLY:
             w1_pass(0, 0, s, t, True)
-        gather_codes(1, 0)
-        gather_codes(1, 1)
+        for s in range(2):
+            window = table[1][:].bitcast(U32).indirect(offsets[:, HALF // 16 * s : HALF // 16 * (s + 1)])
+            nc.vector.tensor_copy(v_codes[1][:, HALF * s : HALF * (s + 1)], window)
+        load_w2(1)
+        round_pair("vector", 0)
+        round_pair("scalar", 1)
         nc.gpsimd.memset(wd_sc[:], 0)
         nc.sync.dma_start(out=wd_codes[:], in_=wd_words.rearrange("a p c i -> p a (c i)").bitcast(I32))
         for q in range(4):
             nc.sync.dma_start(out=wd_sc[32 * q : 32 * q + 4, :, :], in_=wd_scales[:, 4 * q : 4 * q + 4, :].rearrange("a r c -> r a c").bitcast(I32))
-        cast_pair("vector", 0)
-        cast_pair("scalar", 1)
-        load_w2(1)
         quantize_pair(0)
         quantize_pair(1)
+
         for s in range(2):
             for t in range(PACK):
-                w1_pass(1, 0, s, t, (s, t) not in early)
-                if (s, t) not in early:
+                w1_pass(1, 0, s, t, (s, t) not in EARLY)
+                if (s, t) not in EARLY:
                     w1_pass(0, 0, s, t, False)
                 bound(0, s, t)
-        cast_w1("vector", 0, 1, 0, 128)
+        round_w1("vector", 0, 1, 0, P)
         quantize_w1(0, 1)
+        nc.gpsimd.tensor_copy(gain_late[:], gain[:])
         apply_gain(0, 0)
-        cast_w1("vector", 1, 1, 0, 92)
-        cast_w1("scalar", 1, 1, 92, 128)
-        quantize_h(0, 0)
+        round_w1("vector", 1, 1, 0, VECTOR_GROUPS)
+        round_w1("scalar", 1, 1, VECTOR_GROUPS, P)
         quantize_w1(1, 1)
-        cast_w2("scalar", 0, 0, 512)
+        quantize_h(0, 0)
+        round_w2("scalar", 0)
+
         for s in range(2):
             for t in range(PACK):
                 w1_pass(0, 1, s, t, True)
                 w1_pass(1, 1, s, t, False)
                 bound(1, s, t)
         apply_gain(0, 1)
-        cast_w2("vector", 1, 0, 512)
+        round_w2("vector", 1)
         quantize_h(0, 1)
         quantize_w2(0)
-        for s in range(2):
-            for n in range(4):
-                if (s, n) != (1, 3):
-                    direct(s, n)
+        for i in range(BANKS):
+            direct_product(i // 4, i % 4)
         apply_gain(1, 0)
         quantize_w2(1)
         quantize_h(1, 0)
+
         make_gate(0, 0)
-        direct(1, 3)
+        direct_product(1, 3)
         for n in range(4):
             make_gate((n + 1) // 4, (n + 1) % 4)
-            w2_pass(n // 2, 0, n, bank_of(3, 0, n), True)
-            w2_pass(1 - n // 2, 0, n, bank_of(3, 0, n), False)
+            w2_product(0, n, n // 2)
         for n in range(1, 4):
             make_gate(1, n)
         apply_gain(1, 1)
-        finish(0, 0, bank_of(3, 0, 0))
+        finish(0, 0)
         quantize_h(1, 1)
         for n in range(1, 4):
-            finish(0, n, bank_of(3, 0, n))
+            finish(0, n)
         for n in range(4):
-            w2_pass(1, 1, n, bank_of(3, 1, n), True)
-            w2_pass(0, 1, n, bank_of(3, 1, n), False)
-            finish(1, n, bank_of(3, 1, n))
+            w2_product(1, n, 1)
+            finish(1, n)

@@ -24,8 +24,9 @@ HALF = S // 2
 SLOT = 8192
 EDGE = 64
 BANKS = 7
-GPSIMD_COLUMNS = 128
+GPSIMD_COLUMNS = {(0, 0): 128, (0, 1): 128, (1, 0): 128, (1, 1): 224}
 VECTOR_GROUPS = 92
+VECTOR_COLUMNS = 368
 EARLY = [(0, 0), (0, 1), (0, 2), (0, 3), (1, 0)]
 
 
@@ -50,7 +51,8 @@ def tile_list_aligned_error_gate_kernel(tc, tab_words, tab_scales, offs, w1, g, 
 
         w1_at = {(0, 0): 4 * SLOT, (1, 0): scales_at + T - EDGE, (0, 1): SLOT, (1, 1): 0}
         w1_raw = {k: stage.tile([P, PACK, PASS], F32, name="w1_raw%d%d" % k, offset=v) for k, v in w1_at.items()}
-        w2_raw = [stage.tile([P, PACK, N], F32, name=f"w2_raw{b}", offset=(w1_at[0, 0], table_at[1])[b]) for b in range(2)]
+        w2_parts = {"whole": (0, 0, N, w1_at[0, 0]), "first": (1, 0, VECTOR_COLUMNS, table_at[1]), "rest": (1, VECTOR_COLUMNS, N, table_at[1] + 16 * VECTOR_COLUMNS)}
+        w2_raw = {k: stage.tile([P, PACK, c1 - c0], F32, name=f"w2_raw_{k}", offset=at) for k, (b, c0, c1, at) in w2_parts.items()}
         wd_codes = stage.tile([P, 2, N], I32, name="wd_codes", offset=w1_at[1, 0], align_bytes=64)
         v_codes = [keep.tile([P, S], U32, name=f"v_codes{a}", align_bytes=64) for a in range(2)]
         picked_sc = keep.tile([P, S], U8, name="picked_sc", align_bytes=64)
@@ -62,25 +64,31 @@ def tile_list_aligned_error_gate_kernel(tc, tab_words, tab_scales, offs, w1, g, 
         w1_bf = {k: stage.tile([P, PACK, P, PACK], BF16, name="w1_bf%d%d" % k, offset=v, align_bytes=64) for k, v in bf_at.items()}
         gain_late = stage.tile([P, 2, PACK], F32, name="gain_late", offset=bf_at[0, 1])
         w1_pair = [keep.tile([P, 2, P, PACK], BF16, name=f"w1_pair{u}", align_bytes=64) for u in range(2)]
-        w2_bf_at = (8 * SLOT, 6 * SLOT)
+        w2_bf_at = (8 * SLOT, 12 * SLOT)
         w2_bf = [stage.tile([P, N * PACK], BF16, name=f"w2_bf{b}", offset=w2_bf_at[b], align_bytes=64) for b in range(2)]
         w1_codes = {(a, b): keep.tile([P, PASS], U32, name=f"w1_codes{a}{b}", align_bytes=64) for a in range(2) for b in range(2)}
         w1_sc = {(a, b): keep.tile([P, PASS], U8, name=f"w1_sc{a}{b}", align_bytes=64) for a in range(2) for b in range(2)}
         w2_codes = [stage.tile([P, N], U32, name=f"w2_codes{b}", offset=(table_at[1] + 4 * HALF, w2_bf_at[0])[b], align_bytes=64) for b in range(2)]
         w2_sc = keep.tile([P, 2 * N], U8, name="w2_sc", align_bytes=64)
-        h_codes = {(b, s): keep.tile([P, HALF], U32, name=f"h_codes{b}{s}", align_bytes=64) for b, s in ((0, 0), (1, 0), (1, 1))}
+        h_codes = {(b, s): keep.tile([P, HALF], U32, name=f"h_codes{b}{s}", align_bytes=64) for b, s in ((0, 0), (1, 0))}
         h_codes[0, 1] = stage.tile([P, HALF], U32, name="h_codes01", offset=table_at[1], align_bytes=64)
         h_sc = [stage.tile([P, S], U8, name="h_sc0", offset=w1_at[1, 1], align_bytes=64), keep.tile([P, S], U8, name="h_sc1", align_bytes=64)]
-        gate = keep.tile([P, N // P, S], F32, name="gate")
-        bounded = {(b, s): keep.tile([P, PACK, HALF], F32, name=f"bounded{b}{s}") for b, s in ((0, 0), (0, 1), (1, 1))}
+        gate = {(s, n): keep.tile([P, HALF], F32, name=f"gate{s}{n}") for s in range(2) for n in range(4) if s + n}
+        gate[0, 0] = stage.tile([P, HALF], F32, name="gate00", offset=11 * SLOT)
+        h_codes[1, 1] = stage.tile([P, HALF], U32, name="h_codes11", offset=11 * SLOT, align_bytes=64)
+        bounded = {(b, s): keep.tile([P, PACK, HALF], F32, name=f"bounded{b}{s}") for b, s in ((0, 0), (0, 1))}
         bounded[1, 0] = stage.tile([P, PACK, HALF], F32, name="bounded10", offset=w1_at[0, 0])
+        bounded[1, 1] = stage.tile([P, PACK, HALF], F32, name="bounded11", offset=table_at[1] + SLOT - EDGE)
         h_at = {(0, 0): w1_at[0, 1], (0, 1): bf_at[1, 1], (1, 0): bf_at[1, 1], (1, 1): w2_bf_at[1]}
         h_bf = {k: stage.tile([P, HALF, PACK], BF16, name="h_bf%d%d" % k, offset=v, align_bytes=64) for k, v in h_at.items()}
         banks = [psum.tile([P, HALF], F32, name=f"bank{i}") for i in range(BANKS)]
         results = [keep.tile([P, HALF], F32, name=f"result{i}") for i in range(8)]
 
+        turns = [(kind, s, i) for kind in range(3) for s in range(2) for i in range(4)][:-1]
+        turns = turns + [(3, 0, i) for i in range(4)] + [(2, 1, 3)] + [(3, 1, i) for i in range(4)]
+
         def bank_of(kind, s, i):
-            return banks[(8 * kind + 4 * s + i) % BANKS]
+            return banks[turns.index((kind, s, i)) % BANKS]
 
         def load_table(a):
             nc.sync.dma_start(out=table[a][:], in_=tab_words[a].rearrange("p t i -> p (t i)").bitcast(I32))
@@ -89,9 +97,10 @@ def tile_list_aligned_error_gate_kernel(tc, tab_words, tab_scales, offs, w1, g, 
             rows = w1[PASS * a : PASS * (a + 1), PASS * b : PASS * (b + 1)]
             nc.sync.dma_start(out=w1_raw[a, b][:], in_=rows.rearrange("(p j) c -> p j c", j=PACK))
 
-        def load_w2(b):
-            rows = w2[PASS * b : PASS * (b + 1), :]
-            nc.sync.dma_start(out=w2_raw[b][:], in_=rows.rearrange("(p j) c -> p j c", j=PACK))
+        def load_w2(part):
+            b, c0, c1, at = w2_parts[part]
+            rows = w2[PASS * b : PASS * (b + 1), c0:c1]
+            nc.sync.dma_start(out=w2_raw[part][:], in_=rows.rearrange("(p j) c -> p j c", j=PACK))
 
         def move_scales(a):
             for q in range(4):
@@ -113,9 +122,10 @@ def tile_list_aligned_error_gate_kernel(tc, tab_words, tab_scales, offs, w1, g, 
             src = w1_raw[1, 0][:].rearrange("p j (m t) -> p m j t", t=PACK)[:, :, :, 2 * u : 2 * u + 2]
             round_on(engine, dst, src)
 
-        def round_w2(engine, b):
-            dst = w2_bf[b][:].rearrange("p (c i j) -> p c j i", i=4, j=PACK)
-            src = w2_raw[b][:].rearrange("p j (c i) -> p c j i", i=4)
+        def round_w2(engine, part):
+            b, c0, c1, at = w2_parts[part]
+            dst = w2_bf[b][:, PACK * c0 : PACK * c1].rearrange("p (c i j) -> p c j i", i=4, j=PACK)
+            src = w2_raw[part][:].rearrange("p j (c i) -> p c j i", i=4)
             round_on(engine, dst, src)
 
         def quantize_w1(a, b):
@@ -158,7 +168,7 @@ def tile_list_aligned_error_gate_kernel(tc, tab_words, tab_scales, offs, w1, g, 
             nc.scalar.activation(out=bounded[b, s][:, t, :], in_=bank_of(b, s, t)[:], func=ACT.Tanh)
 
         def make_gate(s, n):
-            nc.scalar.activation(out=gate[:, n, HALF * s : HALF * (s + 1)], in_=bank_of(2, s, n)[:], func=ACT.Sigmoid)
+            nc.scalar.activation(out=gate[s, n][:], in_=bank_of(2, s, n)[:], func=ACT.Sigmoid)
 
         def gain_part(engine, factors, b, s, c0, c1):
             engine.tensor_tensor(
@@ -169,13 +179,13 @@ def tile_list_aligned_error_gate_kernel(tc, tab_words, tab_scales, offs, w1, g, 
             )
 
         def apply_gain(b, s):
-            gain_part(nc.gpsimd, gain_late, b, s, HALF - GPSIMD_COLUMNS, HALF)
-            gain_part(nc.vector, gain_ps, b, s, 0, HALF - GPSIMD_COLUMNS)
+            gain_part(nc.gpsimd, gain_late, b, s, HALF - GPSIMD_COLUMNS[b, s], HALF)
+            gain_part(nc.vector, gain_ps, b, s, 0, HALF - GPSIMD_COLUMNS[b, s])
 
         def finish(s, n):
             cols = slice(HALF * s, HALF * (s + 1))
             result = results[4 * s + n]
-            nc.vector.tensor_tensor(out=result[:], in0=bank_of(3, s, n)[:], in1=gate[:, n, cols], op=MULT)
+            nc.vector.tensor_tensor(out=result[:], in0=bank_of(3, s, n)[:], in1=gate[s, n][:], op=MULT)
             nc.sync.dma_start(out=out[P * n : P * (n + 1), cols], in_=result[:])
 
         nc.sync.dma_start(offsets[:], offs)
@@ -206,14 +216,15 @@ def tile_list_aligned_error_gate_kernel(tc, tab_words, tab_scales, offs, w1, g, 
         load_w1(1, 1)
         round_w1("scalar", 0, 0, 0, P // 2)
         round_w1("vector", 0, 0, P // 2, P)
-        load_w2(0)
+        load_w2("whole")
         quantize_w1(0, 0)
         for s, t in EARLY:
             w1_pass(0, 0, s, t, True)
         for s in range(2):
             window = table[1][:].bitcast(U32).indirect(offsets[:, HALF // 16 * s : HALF // 16 * (s + 1)])
             nc.vector.tensor_copy(v_codes[1][:, HALF * s : HALF * (s + 1)], window)
-        load_w2(1)
+        load_w2("first")
+        load_w2("rest")
         round_pair("vector", 0)
         round_pair("scalar", 1)
         nc.gpsimd.memset(wd_sc[:], 0)
@@ -237,15 +248,17 @@ def tile_list_aligned_error_gate_kernel(tc, tab_words, tab_scales, offs, w1, g, 
         round_w1("scalar", 1, 1, VECTOR_GROUPS, P)
         quantize_w1(1, 1)
         quantize_h(0, 0)
-        round_w2("scalar", 0)
+        round_w2("scalar", "whole")
 
         for s in range(2):
             for t in range(PACK):
                 w1_pass(0, 1, s, t, True)
                 w1_pass(1, 1, s, t, False)
                 bound(1, s, t)
+            if s == 0:
+                round_w2("scalar", "rest")
         apply_gain(0, 1)
-        round_w2("vector", 1)
+        round_w2("vector", "first")
         quantize_h(0, 1)
         quantize_w2(0)
         for i in range(BANKS):
@@ -254,17 +267,18 @@ def tile_list_aligned_error_gate_kernel(tc, tab_words, tab_scales, offs, w1, g, 
         quantize_w2(1)
         quantize_h(1, 0)
 
-        make_gate(0, 0)
-        direct_product(1, 3)
         for n in range(4):
-            make_gate((n + 1) // 4, (n + 1) % 4)
+            make_gate(0, n)
             w2_product(0, n, n // 2)
+        make_gate(1, 0)
+        direct_product(1, 3)
         for n in range(1, 4):
             make_gate(1, n)
         apply_gain(1, 1)
-        finish(0, 0)
+        for n in range(3):
+            finish(0, n)
         quantize_h(1, 1)
-        for n in range(1, 4):
+        for n in range(3, 4):
             finish(0, n)
         for n in range(4):
             w2_product(1, n, 1)

@@ -24,9 +24,9 @@ HALF = S // 2
 SLOT = 8192
 EDGE = 64
 BANKS = 7
-GPSIMD_COLUMNS = {(0, 0): 128, (0, 1): 128, (1, 0): 128, (1, 1): 224}
+GPSIMD_COLUMNS = {(0, 0): 160, (0, 1): 160, (1, 0): 160, (1, 1): 256}
 VECTOR_GROUPS = 92
-VECTOR_COLUMNS = 368
+VECTOR_COLUMNS = 384
 EARLY = [(0, 0), (0, 1), (0, 2), (0, 3), (1, 0)]
 
 
@@ -73,8 +73,8 @@ def tile_list_aligned_error_gate_kernel(tc, tab_words, tab_scales, offs, w1, g, 
         h_codes = {(b, s): keep.tile([P, HALF], U32, name=f"h_codes{b}{s}", align_bytes=64) for b, s in ((0, 0), (1, 0))}
         h_codes[0, 1] = stage.tile([P, HALF], U32, name="h_codes01", offset=table_at[1], align_bytes=64)
         h_sc = [stage.tile([P, S], U8, name="h_sc0", offset=w1_at[1, 1], align_bytes=64), keep.tile([P, S], U8, name="h_sc1", align_bytes=64)]
-        gate = {(s, n): keep.tile([P, HALF], F32, name=f"gate{s}{n}") for s in range(2) for n in range(4) if s + n}
-        gate[0, 0] = stage.tile([P, HALF], F32, name="gate00", offset=11 * SLOT)
+        gate = {(s, n): keep.tile([P, HALF], F32, name=f"gate{s}{n}") for s in range(2) for n in range(4) if (s, n) != (0, 1)}
+        gate[0, 1] = stage.tile([P, HALF], F32, name="gate01", offset=11 * SLOT)
         h_codes[1, 1] = stage.tile([P, HALF], U32, name="h_codes11", offset=11 * SLOT, align_bytes=64)
         bounded = {(b, s): keep.tile([P, PACK, HALF], F32, name=f"bounded{b}{s}") for b, s in ((0, 0), (0, 1))}
         bounded[1, 0] = stage.tile([P, PACK, HALF], F32, name="bounded10", offset=w1_at[0, 0])
@@ -82,10 +82,11 @@ def tile_list_aligned_error_gate_kernel(tc, tab_words, tab_scales, offs, w1, g, 
         h_at = {(0, 0): w1_at[0, 1], (0, 1): bf_at[1, 1], (1, 0): bf_at[1, 1], (1, 1): w2_bf_at[1]}
         h_bf = {k: stage.tile([P, HALF, PACK], BF16, name="h_bf%d%d" % k, offset=v, align_bytes=64) for k, v in h_at.items()}
         banks = [psum.tile([P, HALF], F32, name=f"bank{i}") for i in range(BANKS)]
-        results = [keep.tile([P, HALF], F32, name=f"result{i}") for i in range(8)]
+        results = {i: keep.tile([P, HALF], F32, name=f"result{i}") for i in range(8) if i != 3}
+        results[3] = stage.tile([P, HALF], F32, name="result3", offset=bf_at[0, 1])
 
         turns = [(kind, s, i) for kind in range(3) for s in range(2) for i in range(4)][:-1]
-        turns = turns + [(3, 0, i) for i in range(4)] + [(2, 1, 3)] + [(3, 1, i) for i in range(4)]
+        turns = turns + [(3, 0, i) for i in range(4)] + [(2, 1, 3)] + [(3, 1, i) for i in (2, 3, 0, 1)]
 
         def bank_of(kind, s, i):
             return banks[turns.index((kind, s, i)) % BANKS]
@@ -281,5 +282,5 @@ def tile_list_aligned_error_gate_kernel(tc, tab_words, tab_scales, offs, w1, g, 
         for n in range(3, 4):
             finish(0, n)
         for n in range(4):
-            w2_product(1, n, 1)
+            w2_product(1, n, n // 2)
             finish(1, n)

@@ -24,7 +24,7 @@ HALF = S // 2
 SLOT = 8192
 EDGE = 64
 BANKS = 7
-GPSIMD_COLUMNS = {(0, 0): 160, (0, 1): 160, (1, 0): 160, (1, 1): 256}
+GPSIMD_COLUMNS = {(0, 0): 128, (0, 1): 160, (1, 0): 160, (1, 1): 256}
 VECTOR_GROUPS = 92
 VECTOR_COLUMNS = 384
 EARLY = [(0, 0), (0, 1), (0, 2), (0, 3), (1, 0)]
@@ -68,16 +68,16 @@ def tile_list_aligned_error_gate_kernel(tc, tab_words, tab_scales, offs, w1, g, 
         w2_bf = [stage.tile([P, N * PACK], BF16, name=f"w2_bf{b}", offset=w2_bf_at[b], align_bytes=64) for b in range(2)]
         w1_codes = {(a, b): keep.tile([P, PASS], U32, name=f"w1_codes{a}{b}", align_bytes=64) for a in range(2) for b in range(2)}
         w1_sc = {(a, b): keep.tile([P, PASS], U8, name=f"w1_sc{a}{b}", align_bytes=64) for a in range(2) for b in range(2)}
-        w2_codes = [stage.tile([P, N], U32, name=f"w2_codes{b}", offset=(table_at[1] + 4 * HALF, w2_bf_at[0])[b], align_bytes=64) for b in range(2)]
+        w2_codes = [stage.tile([P, N], U32, name=f"w2_codes{b}", offset=(13 * SLOT, w2_bf_at[0])[b], align_bytes=64) for b in range(2)]
         w2_sc = keep.tile([P, 2 * N], U8, name="w2_sc", align_bytes=64)
         h_codes = {(b, s): keep.tile([P, HALF], U32, name=f"h_codes{b}{s}", align_bytes=64) for b, s in ((0, 0), (1, 0))}
-        h_codes[0, 1] = stage.tile([P, HALF], U32, name="h_codes01", offset=table_at[1], align_bytes=64)
+        h_codes[0, 1] = stage.tile([P, HALF], U32, name="h_codes01", offset=w1_at[0, 0] + EDGE, align_bytes=64)
         h_sc = [stage.tile([P, S], U8, name="h_sc0", offset=w1_at[1, 1], align_bytes=64), keep.tile([P, S], U8, name="h_sc1", align_bytes=64)]
         gate = {(s, n): keep.tile([P, HALF], F32, name=f"gate{s}{n}") for s in range(2) for n in range(4) if (s, n) != (0, 1)}
         gate[0, 1] = stage.tile([P, HALF], F32, name="gate01", offset=11 * SLOT)
         h_codes[1, 1] = stage.tile([P, HALF], U32, name="h_codes11", offset=11 * SLOT, align_bytes=64)
         bounded = {(b, s): keep.tile([P, PACK, HALF], F32, name=f"bounded{b}{s}") for b, s in ((0, 0), (0, 1))}
-        bounded[1, 0] = stage.tile([P, PACK, HALF], F32, name="bounded10", offset=w1_at[0, 0])
+        bounded[1, 0] = stage.tile([P, PACK, HALF], F32, name="bounded10", offset=w1_at[0, 0] - SLOT + EDGE)
         bounded[1, 1] = stage.tile([P, PACK, HALF], F32, name="bounded11", offset=table_at[1] + SLOT - EDGE)
         h_at = {(0, 0): w1_at[0, 1], (0, 1): bf_at[1, 1], (1, 0): bf_at[1, 1], (1, 1): w2_bf_at[1]}
         h_bf = {k: stage.tile([P, HALF, PACK], BF16, name="h_bf%d%d" % k, offset=v, align_bytes=64) for k, v in h_at.items()}
@@ -259,9 +259,9 @@ def tile_list_aligned_error_gate_kernel(tc, tab_words, tab_scales, offs, w1, g, 
             if s == 0:
                 round_w2("scalar", "rest")
         apply_gain(0, 1)
-        round_w2("vector", "first")
-        quantize_h(0, 1)
         quantize_w2(0)
+        quantize_h(0, 1)
+        round_w2("vector", "first")
         for i in range(BANKS):
             direct_product(i // 4, i % 4)
         apply_gain(1, 0)

@@ -21,13 +21,15 @@ P = 128
 PACK = 4
 PASS = P * PACK
 HALF = S // 2
+QUARTER = S // 4
 SLOT = 8192
 EDGE = 64
 BANKS = 7
 GPSIMD_COLUMNS = {(0, 0): 128, (0, 1): 160, (1, 0): 160, (1, 1): 256}
-VECTOR_GROUPS = 92
+VECTOR_GROUPS = 80
 VECTOR_COLUMNS = 384
-EARLY = [(0, 0), (0, 1), (0, 2), (0, 3), (1, 0)]
+HEAD_GROUPS = 84
+EARLY = []
 
 
 def tile_list_aligned_error_gate_kernel(tc, tab_words, tab_scales, offs, w1, g, w2, wd_words, wd_scales, out):
@@ -40,30 +42,29 @@ def tile_list_aligned_error_gate_kernel(tc, tab_words, tab_scales, offs, w1, g, 
         offsets = keep.tile([P, S // 16], U16, name="offsets")
         warm_in = keep.tile([P, 16], F32, name="warm_in")
         warm_out = keep.tile([P, 16], F32, name="warm_out")
-        table_at = (0, 5 * SLOT)
-        table = [stage.tile([P, T], I32, name=f"table{a}", offset=table_at[a], align_bytes=64) for a in range(2)]
         scales_at = 2 * SLOT - EDGE
+        table_at = (0, scales_at + T - EDGE)
+        table = [stage.tile([P, T], I32, name=f"table{a}", offset=table_at[a], align_bytes=64) for a in range(2)]
         table_sc = stage.tile([P, T // 4], I32, name="table_sc", offset=scales_at, align_bytes=64)
         gain = keep.tile([P, 2, PACK], F32, name="gain")
         gain_rows = keep.tile([P, PASS], F32, name="gain_rows")
         ident = keep.tile([P, P], F32, name="ident")
         gain_ps = psum.tile([P, P, PACK], F32, name="gain_ps")
 
-        w1_at = {(0, 0): 4 * SLOT, (1, 0): scales_at + T - EDGE, (0, 1): SLOT, (1, 1): 0}
+        w1_at = {(0, 0): 4 * SLOT, (1, 0): 5 * SLOT, (0, 1): SLOT, (1, 1): 0}
         w1_raw = {k: stage.tile([P, PACK, PASS], F32, name="w1_raw%d%d" % k, offset=v) for k, v in w1_at.items()}
-        w2_parts = {"whole": (0, 0, N, w1_at[0, 0]), "first": (1, 0, VECTOR_COLUMNS, table_at[1]), "rest": (1, VECTOR_COLUMNS, N, table_at[1] + 16 * VECTOR_COLUMNS)}
+        w2_parts = {"whole": (0, 0, N, w1_at[0, 0]), "first": (1, 0, VECTOR_COLUMNS, w1_at[1, 0]), "rest": (1, VECTOR_COLUMNS, N, w1_at[1, 0] + 16 * VECTOR_COLUMNS)}
         w2_raw = {k: stage.tile([P, PACK, c1 - c0], F32, name=f"w2_raw_{k}", offset=at) for k, (b, c0, c1, at) in w2_parts.items()}
-        wd_codes = stage.tile([P, 2, N], I32, name="wd_codes", offset=w1_at[1, 0], align_bytes=64)
+        wd_codes = stage.tile([P, 2, N], I32, name="wd_codes", offset=table_at[1], align_bytes=64)
         v_codes = [keep.tile([P, S], U32, name=f"v_codes{a}", align_bytes=64) for a in range(2)]
         picked_sc = keep.tile([P, S], U8, name="picked_sc", align_bytes=64)
         moved_sc = [keep.tile([P, S // 4], I32, name=f"moved_sc{a}", align_bytes=64) for a in range(2)]
         v_sc = [moved_sc[a][:].bitcast(U8) for a in range(2)]
 
-        wd_sc = stage.tile([P, 2, N // 4], I32, name="wd_sc", offset=w1_at[1, 0] + 8 * N, align_bytes=64)
-        bf_at = {(0, 0): 7 * SLOT, (0, 1): 10 * SLOT, (1, 1): 9 * SLOT}
+        bf_at = {(0, 0): 7 * SLOT, (1, 0): 7 * SLOT + SLOT // 2, (0, 1): 10 * SLOT, (1, 1): 9 * SLOT}
+        wd_sc = stage.tile([P, 2, N // 4], I32, name="wd_sc", offset=bf_at[1, 0], align_bytes=64)
         w1_bf = {k: stage.tile([P, PACK, P, PACK], BF16, name="w1_bf%d%d" % k, offset=v, align_bytes=64) for k, v in bf_at.items()}
-        gain_late = stage.tile([P, 2, PACK], F32, name="gain_late", offset=bf_at[0, 1])
-        w1_pair = [keep.tile([P, 2, P, PACK], BF16, name=f"w1_pair{u}", align_bytes=64) for u in range(2)]
+        gain_late = stage.tile([P, 2, PACK], F32, name="gain_late", offset=w1_at[0, 1])
         w2_bf_at = (8 * SLOT, 12 * SLOT)
         w2_bf = [stage.tile([P, N * PACK], BF16, name=f"w2_bf{b}", offset=w2_bf_at[b], align_bytes=64) for b in range(2)]
         w1_codes = {(a, b): keep.tile([P, PASS], U32, name=f"w1_codes{a}{b}", align_bytes=64) for a in range(2) for b in range(2)}
@@ -72,18 +73,18 @@ def tile_list_aligned_error_gate_kernel(tc, tab_words, tab_scales, offs, w1, g, 
         w2_sc = keep.tile([P, 2 * N], U8, name="w2_sc", align_bytes=64)
         h_codes = {(b, s): keep.tile([P, HALF], U32, name=f"h_codes{b}{s}", align_bytes=64) for b, s in ((0, 0), (1, 0))}
         h_codes[0, 1] = stage.tile([P, HALF], U32, name="h_codes01", offset=w1_at[0, 0] + EDGE, align_bytes=64)
-        h_sc = [stage.tile([P, S], U8, name="h_sc0", offset=w1_at[1, 1], align_bytes=64), keep.tile([P, S], U8, name="h_sc1", align_bytes=64)]
+        h_sc = [keep.tile([P, S], U8, name=f"h_sc{b}", align_bytes=64) for b in range(2)]
         gate = {(s, n): keep.tile([P, HALF], F32, name=f"gate{s}{n}") for s in range(2) for n in range(4) if (s, n) != (0, 1)}
         gate[0, 1] = stage.tile([P, HALF], F32, name="gate01", offset=11 * SLOT)
         h_codes[1, 1] = stage.tile([P, HALF], U32, name="h_codes11", offset=11 * SLOT, align_bytes=64)
         bounded = {(b, s): keep.tile([P, PACK, HALF], F32, name=f"bounded{b}{s}") for b, s in ((0, 0), (0, 1))}
         bounded[1, 0] = stage.tile([P, PACK, HALF], F32, name="bounded10", offset=w1_at[0, 0] - SLOT + EDGE)
-        bounded[1, 1] = stage.tile([P, PACK, HALF], F32, name="bounded11", offset=table_at[1] + SLOT - EDGE)
-        h_at = {(0, 0): w1_at[0, 1], (0, 1): bf_at[1, 1], (1, 0): bf_at[1, 1], (1, 1): w2_bf_at[1]}
+        bounded[1, 1] = stage.tile([P, PACK, HALF], F32, name="bounded11", offset=w1_at[1, 0] + SLOT - EDGE)
+        h_at = {(0, 0): 14 * SLOT, (0, 1): 14 * SLOT, (1, 0): 14 * SLOT, (1, 1): w2_bf_at[1]}
         h_bf = {k: stage.tile([P, HALF, PACK], BF16, name="h_bf%d%d" % k, offset=v, align_bytes=64) for k, v in h_at.items()}
         banks = [psum.tile([P, HALF], F32, name=f"bank{i}") for i in range(BANKS)]
         results = {i: keep.tile([P, HALF], F32, name=f"result{i}") for i in range(8) if i != 3}
-        results[3] = stage.tile([P, HALF], F32, name="result3", offset=bf_at[0, 1])
+        results[3] = stage.tile([P, HALF], F32, name="result3", offset=w1_at[0, 1])
 
         turns = [(kind, s, i) for kind in range(3) for s in range(2) for i in range(4)][:-1]
         turns = turns + [(3, 0, i) for i in range(4)] + [(2, 1, 3)] + [(3, 1, i) for i in (2, 3, 0, 1)]
@@ -118,11 +119,6 @@ def tile_list_aligned_error_gate_kernel(tc, tab_words, tab_scales, offs, w1, g, 
             src = w1_raw[a, b][:, :, PACK * m0 : PACK * m1].rearrange("p j (m t) -> p m j t", t=PACK)
             round_on(engine, dst, src)
 
-        def round_pair(engine, u):
-            dst = w1_pair[u][:].rearrange("p t m j -> p m j t")
-            src = w1_raw[1, 0][:].rearrange("p j (m t) -> p m j t", t=PACK)[:, :, :, 2 * u : 2 * u + 2]
-            round_on(engine, dst, src)
-
         def round_w2(engine, part):
             b, c0, c1, at = w2_parts[part]
             dst = w2_bf[b][:, PACK * c0 : PACK * c1].rearrange("p (c i j) -> p c j i", i=4, j=PACK)
@@ -131,10 +127,6 @@ def tile_list_aligned_error_gate_kernel(tc, tab_words, tab_scales, offs, w1, g, 
 
         def quantize_w1(a, b):
             nc.vector.quantize_mx(out=w1_codes[a, b][:].bitcast(E4M3), scales=w1_sc[a, b][:], in_=w1_bf[a, b][:].rearrange("p t m j -> p (t m j)"))
-
-        def quantize_pair(u):
-            cols = slice(2 * P * u, 2 * P * (u + 1))
-            nc.vector.quantize_mx(out=w1_codes[1, 0][:, cols].bitcast(E4M3), scales=w1_sc[1, 0][:, cols], in_=w1_pair[u][:].rearrange("p t m j -> p (t m j)"))
 
         def quantize_w2(b):
             nc.vector.quantize_mx(out=w2_codes[b][:].bitcast(E4M3), scales=w2_sc[:, N * b : N * (b + 1)], in_=w2_bf[b][:])
@@ -152,6 +144,20 @@ def tile_list_aligned_error_gate_kernel(tc, tab_words, tab_scales, offs, w1, g, 
         def w1_pass(a, b, s, t, first):
             cols = slice(P * t, P * (t + 1))
             table_pass(bank_of(b, s, t), w1_codes[a, b][:, cols], w1_sc[a, b][:, cols], a, s, first)
+
+        def quarter_pass(a, u, t, first, last):
+            cols, picked = slice(P * t, P * (t + 1)), slice(QUARTER * u, QUARTER * (u + 1))
+            nc.tensor.matmul_mx(out=bank_of(0, 0, 2 * u + t // 2)[:, QUARTER * (t % 2) : QUARTER * (t % 2 + 1)],
+                                lhsT=w1_codes[a, 0][:, cols].bitcast(E4M3), lhsT_scale=w1_sc[a, 0][:, cols],
+                                rhs=v_codes[a][:, picked].bitcast(E5M2), rhs_scale=v_sc[a][:, picked],
+                                start=first, stop=last)
+
+        def bound_quarter(u, pair):
+            nc.scalar.activation(out=bounded[0, 0][:, 2 * pair : 2 * pair + 2, QUARTER * u : QUARTER * (u + 1)],
+                                 in_=bank_of(0, 0, 2 * u + pair)[:].rearrange("p (t c) -> p t c", t=2), func=ACT.Tanh)
+
+        def gather_words(a, c0, c1):
+            nc.vector.tensor_copy(v_codes[a][:, c0:c1], table[a][:].bitcast(U32).indirect(offsets[:, c0 // 16 : c1 // 16]))
 
         def direct_product(s, n):
             cols = slice(P * n, P * (n + 1))
@@ -207,48 +213,54 @@ def tile_list_aligned_error_gate_kernel(tc, tab_words, tab_scales, offs, w1, g, 
 
         load_table(0)
         load_w1(0, 0)
-        load_table(1)
+        load_w1(1, 0)
         nc.vector.tensor_copy(picked_sc[:], table_sc[:].bitcast(U8).indirect(offsets[:]))
         move_scales(0)
-        load_w1(1, 0)
+        load_table(1)
         move_scales(1)
         load_w1(0, 1)
-        nc.vector.tensor_copy(v_codes[0][:], table[0][:].bitcast(U32).indirect(offsets[:]))
+        gather_words(0, 0, S)
         load_w1(1, 1)
         round_w1("scalar", 0, 0, 0, P // 2)
         round_w1("vector", 0, 0, P // 2, P)
         load_w2("whole")
         quantize_w1(0, 0)
+        round_w1("vector", 1, 0, 0, HEAD_GROUPS)
+        round_w1("scalar", 1, 0, HEAD_GROUPS, P)
+        quantize_w1(1, 0)
+        for u in range(2):
+            for t in range(PACK):
+                quarter_pass(0, u, t, t % 2 == 0, False)
         for s, t in EARLY:
             w1_pass(0, 0, s, t, True)
-        for s in range(2):
-            window = table[1][:].bitcast(U32).indirect(offsets[:, HALF // 16 * s : HALF // 16 * (s + 1)])
-            nc.vector.tensor_copy(v_codes[1][:, HALF * s : HALF * (s + 1)], window)
         load_w2("first")
         load_w2("rest")
-        round_pair("vector", 0)
-        round_pair("scalar", 1)
+        gather_words(1, 0, QUARTER)
+        gather_words(1, QUARTER, HALF)
+        gather_words(1, HALF, S)
         nc.gpsimd.memset(wd_sc[:], 0)
         nc.sync.dma_start(out=wd_codes[:], in_=wd_words.rearrange("a p c i -> p a (c i)").bitcast(I32))
         for q in range(4):
             nc.sync.dma_start(out=wd_sc[32 * q : 32 * q + 4, :, :], in_=wd_scales[:, 4 * q : 4 * q + 4, :].rearrange("a r c -> r a c").bitcast(I32))
-        quantize_pair(0)
-        quantize_pair(1)
 
-        for s in range(2):
+        for u in range(2):
             for t in range(PACK):
-                w1_pass(1, 0, s, t, (s, t) not in EARLY)
-                if (s, t) not in EARLY:
-                    w1_pass(0, 0, s, t, False)
-                bound(0, s, t)
+                quarter_pass(1, u, t, False, t % 2 == 1)
+                if t % 2 == 1:
+                    bound_quarter(u, t // 2)
+        for t in range(PACK):
+            w1_pass(1, 0, 1, t, (1, t) not in EARLY)
+            if (1, t) not in EARLY:
+                w1_pass(0, 0, 1, t, False)
+            bound(0, 1, t)
         round_w1("vector", 0, 1, 0, P)
-        quantize_w1(0, 1)
         nc.gpsimd.tensor_copy(gain_late[:], gain[:])
         apply_gain(0, 0)
+        quantize_w1(0, 1)
         round_w1("vector", 1, 1, 0, VECTOR_GROUPS)
         round_w1("scalar", 1, 1, VECTOR_GROUPS, P)
-        quantize_w1(1, 1)
         quantize_h(0, 0)
+        quantize_w1(1, 1)
         round_w2("scalar", "whole")
 
         for s in range(2):

@@ -26,8 +26,8 @@ SLOT = 8192
 EDGE = 64
 BANKS = 7
 GPSIMD_COLUMNS = {(0, 0): 128, (0, 1): 160, (1, 0): 160, (1, 1): 256}
-VECTOR_GROUPS = 80
-VECTOR_COLUMNS = 384
+VECTOR_GROUPS = 68
+VECTOR_COLUMNS = 464
 HEAD_GROUPS = 84
 EARLY = []
 
@@ -112,17 +112,17 @@ def tile_list_aligned_error_gate_kernel(tc, tab_words, tab_scales, offs, w1, g, 
             if engine == "vector":
                 nc.vector.tensor_copy(out=dst, in_=src)
             else:
-                nc.scalar.activation(out=dst, in_=src, func=ACT.Copy)
+                nc.scalar.copy(out=dst, in_=src)
 
         def round_w1(engine, a, b, m0, m1):
-            dst = w1_bf[a, b][:, :, m0:m1, :].rearrange("p t m j -> p m j t")
-            src = w1_raw[a, b][:, :, PACK * m0 : PACK * m1].rearrange("p j (m t) -> p m j t", t=PACK)
+            dst = w1_bf[a, b][:, :, m0:m1, :].rearrange("p (u e) m j -> p m u j e", e=2)
+            src = w1_raw[a, b][:, :, PACK * m0 : PACK * m1].rearrange("p j (m u e) -> p m u j e", u=2, e=2)
             round_on(engine, dst, src)
 
         def round_w2(engine, part):
             b, c0, c1, at = w2_parts[part]
-            dst = w2_bf[b][:, PACK * c0 : PACK * c1].rearrange("p (c i j) -> p c j i", i=4, j=PACK)
-            src = w2_raw[part][:].rearrange("p j (c i) -> p c j i", i=4)
+            dst = w2_bf[b][:, PACK * c0 : PACK * c1].rearrange("p (c i j) -> p c j i", i=2, j=PACK)
+            src = w2_raw[part][:].rearrange("p j (c i) -> p c j i", i=2)
             round_on(engine, dst, src)
 
         def quantize_w1(a, b):
@@ -179,9 +179,9 @@ def tile_list_aligned_error_gate_kernel(tc, tab_words, tab_scales, offs, w1, g, 
 
         def gain_part(engine, factors, b, s, c0, c1):
             engine.tensor_tensor(
-                out=h_bf[b, s][:, c0:c1, :].rearrange("p (c i) t -> p c t i", i=4),
-                in0=bounded[b, s][:, :, c0:c1].rearrange("p t (c i) -> p c t i", i=4),
-                in1=factors[:, b, :].unsqueeze(1).unsqueeze(3).to_broadcast([P, (c1 - c0) // 4, PACK, 4]),
+                out=h_bf[b, s][:, c0:c1, :].rearrange("p (c i) t -> p c t i", i=2),
+                in0=bounded[b, s][:, :, c0:c1].rearrange("p t (c i) -> p c t i", i=2),
+                in1=factors[:, b, :].unsqueeze(1).unsqueeze(3).to_broadcast([P, (c1 - c0) // 2, PACK, 2]),
                 op=MULT,
             )
 

from contextlib import ExitStack

import concourse.mybir as mybir
from concourse.masks import make_identity

K, T, S, H, N = 1024, 2048, 1024, 1024, 512
FLOPS = 2 * S * (K * H + H * N + K * N)

F32 = mybir.dt.float32
BF16 = mybir.dt.bfloat16
I32 = mybir.dt.int32
U32 = mybir.dt.uint32
U16 = mybir.dt.uint16
U8 = mybir.dt.uint8
E4M3 = mybir.dt.float8_e4m3fn_x4
E5M2 = mybir.dt.float8_e5m2_x4
ACT = mybir.ActivationFunctionType
MULT = mybir.AluOpType.mult

P = 128
PACK = 4
PASS = P * PACK
HALF = S // 2
QUARTER = S // 4
SLOT = 8192
EDGE = 64
BANKS = 7
GPSIMD_COLUMNS = {(0, 0): 128, (0, 1): 160, (1, 0): 160, (1, 1): 256}
VECTOR_GROUPS = 68
VECTOR_COLUMNS = 464
HEAD_GROUPS = 84
EARLY = []


def tile_list_aligned_error_gate_kernel(tc, tab_words, tab_scales, offs, w1, g, w2, wd_words, wd_scales, out):
    nc = tc.nc
    with ExitStack() as ctx:
        keep = ctx.enter_context(tc.tile_pool(name="keep", bufs=1))
        stage = ctx.enter_context(tc.tile_pool(name="stage", bufs=1))
        psum = ctx.enter_context(tc.psum_pool(name="psum", bufs=1))

        offsets = keep.tile([P, S // 16], U16, name="offsets")
        warm_in = keep.tile([P, 16], F32, name="warm_in")
        warm_out = keep.tile([P, 16], F32, name="warm_out")
        scales_at = 2 * SLOT - EDGE
        table_at = (0, scales_at + T - EDGE)
        table = [stage.tile([P, T], I32, name=f"table{a}", offset=table_at[a], align_bytes=64) for a in range(2)]
        table_sc = stage.tile([P, T // 4], I32, name="table_sc", offset=scales_at, align_bytes=64)
        gain = keep.tile([P, 2, PACK], F32, name="gain")
        gain_rows = keep.tile([P, PASS], F32, name="gain_rows")
        ident = keep.tile([P, P], F32, name="ident")
        gain_ps = psum.tile([P, P, PACK], F32, name="gain_ps")

        w1_at = {(0, 0): 4 * SLOT, (1, 0): 5 * SLOT, (0, 1): SLOT, (1, 1): 0}
        w1_raw = {k: stage.tile([P, PACK, PASS], F32, name="w1_raw%d%d" % k, offset=v) for k, v in w1_at.items()}
        w2_parts = {"whole": (0, 0, N, w1_at[0, 0]), "first": (1, 0, VECTOR_COLUMNS, w1_at[1, 0]), "rest": (1, VECTOR_COLUMNS, N, w1_at[1, 0] + 16 * VECTOR_COLUMNS)}
        w2_raw = {k: stage.tile([P, PACK, c1 - c0], F32, name=f"w2_raw_{k}", offset=at) for k, (b, c0, c1, at) in w2_parts.items()}
        wd_codes = stage.tile([P, 2, N], I32, name="wd_codes", offset=table_at[1], align_bytes=64)
        v_codes = [keep.tile([P, S], U32, name=f"v_codes{a}", align_bytes=64) for a in range(2)]
        picked_sc = keep.tile([P, S], U8, name="picked_sc", align_bytes=64)
        moved_sc = [keep.tile([P, S // 4], I32, name=f"moved_sc{a}", align_bytes=64) for a in range(2)]
        v_sc = [moved_sc[a][:].bitcast(U8) for a in range(2)]

        bf_at = {(0, 0): 7 * SLOT, (1, 0): 7 * SLOT + SLOT // 2, (0, 1): 10 * SLOT, (1, 1): 9 * SLOT}
        wd_sc = stage.tile([P, 2, N // 4], I32, name="wd_sc", offset=bf_at[1, 0], align_bytes=64)
        w1_bf = {k: stage.tile([P, PACK, P, PACK], BF16, name="w1_bf%d%d" % k, offset=v, align_bytes=64) for k, v in bf_at.items()}
        gain_late = stage.tile([P, 2, PACK], F32, name="gain_late", offset=w1_at[0, 1])
        w2_bf_at = (8 * SLOT, 12 * SLOT)
        w2_bf = [stage.tile([P, N * PACK], BF16, name=f"w2_bf{b}", offset=w2_bf_at[b], align_bytes=64) for b in range(2)]
        w1_codes = {(a, b): keep.tile([P, PASS], U32, name=f"w1_codes{a}{b}", align_bytes=64) for a in range(2) for b in range(2)}
        w1_sc = {(a, b): keep.tile([P, PASS], U8, name=f"w1_sc{a}{b}", align_bytes=64) for a in range(2) for b in range(2)}
        w2_codes = [stage.tile([P, N], U32, name=f"w2_codes{b}", offset=(13 * SLOT, w2_bf_at[0])[b], align_bytes=64) for b in range(2)]
        w2_sc = keep.tile([P, 2 * N], U8, name="w2_sc", align_bytes=64)
        h_codes = {(b, s): keep.tile([P, HALF], U32, name=f"h_codes{b}{s}", align_bytes=64) for b, s in ((0, 0), (1, 0))}
        h_codes[0, 1] = stage.tile([P, HALF], U32, name="h_codes01", offset=w1_at[0, 0] + EDGE, align_bytes=64)
        h_sc = [keep.tile([P, S], U8, name=f"h_sc{b}", align_bytes=64) for b in range(2)]
        gate = {(s, n): keep.tile([P, HALF], F32, name=f"gate{s}{n}") for s in range(2) for n in range(4) if (s, n) != (0, 1)}
        gate[0, 1] = stage.tile([P, HALF], F32, name="gate01", offset=11 * SLOT)
        h_codes[1, 1] = stage.tile([P, HALF], U32, name="h_codes11", offset=11 * SLOT, align_bytes=64)
        bounded = {(b, s): keep.tile([P, PACK, HALF], F32, name=f"bounded{b}{s}") for b, s in ((0, 0), (0, 1))}
        bounded[1, 0] = stage.tile([P, PACK, HALF], F32, name="bounded10", offset=w1_at[0, 0] - SLOT + EDGE)
        bounded[1, 1] = stage.tile([P, PACK, HALF], F32, name="bounded11", offset=w1_at[1, 0] + SLOT - EDGE)
        h_at = {(0, 0): 14 * SLOT, (0, 1): 14 * SLOT, (1, 0): 14 * SLOT, (1, 1): w2_bf_at[1]}
        h_bf = {k: stage.tile([P, HALF, PACK], BF16, name="h_bf%d%d" % k, offset=v, align_bytes=64) for k, v in h_at.items()}
        banks = [psum.tile([P, HALF], F32, name=f"bank{i}") for i in range(BANKS)]
        results = {i: keep.tile([P, HALF], F32, name=f"result{i}") for i in range(8) if i != 3}
        results[3] = stage.tile([P, HALF], F32, name="result3", offset=w1_at[0, 1])

        turns = [(kind, s, i) for kind in range(3) for s in range(2) for i in range(4)][:-1]
        turns = turns + [(3, 0, i) for i in range(4)] + [(2, 1, 3)] + [(3, 1, i) for i in (2, 3, 0, 1)]

        def bank_of(kind, s, i):
            return banks[turns.index((kind, s, i)) % BANKS]

        def load_table(a):
            nc.sync.dma_start(out=table[a][:], in_=tab_words[a].rearrange("p t i -> p (t i)").bitcast(I32))

        def load_w1(a, b):
            rows = w1[PASS * a : PASS * (a + 1), PASS * b : PASS * (b + 1)]
            nc.sync.dma_start(out=w1_raw[a, b][:], in_=rows.rearrange("(p j) c -> p j c", j=PACK))

        def load_w2(part):
            b, c0, c1, at = w2_parts[part]
            rows = w2[PASS * b : PASS * (b + 1), c0:c1]
            nc.sync.dma_start(out=w2_raw[part][:], in_=rows.rearrange("(p j) c -> p j c", j=PACK))

        def move_scales(a):
            for q in range(4):
                nc.sync.dma_start(out=moved_sc[a][32 * q : 32 * q + 4, :], in_=picked_sc[16 * a + 4 * q : 16 * a + 4 * q + 4, :].bitcast(I32))

        def round_on(engine, dst, src):
            if engine == "vector":
                nc.vector.tensor_copy(out=dst, in_=src)
            else:
                nc.scalar.copy(out=dst, in_=src)

        def round_w1(engine, a, b, m0, m1):
            dst = w1_bf[a, b][:, :, m0:m1, :].rearrange("p (u e) m j -> p m u j e", e=2)
            src = w1_raw[a, b][:, :, PACK * m0 : PACK * m1].rearrange("p j (m u e) -> p m u j e", u=2, e=2)
            round_on(engine, dst, src)

        def round_w2(engine, part):
            b, c0, c1, at = w2_parts[part]
            dst = w2_bf[b][:, PACK * c0 : PACK * c1].rearrange("p (c i j) -> p c j i", i=2, j=PACK)
            src = w2_raw[part][:].rearrange("p j (c i) -> p c j i", i=2)
            round_on(engine, dst, src)

        def quantize_w1(a, b):
            nc.vector.quantize_mx(out=w1_codes[a, b][:].bitcast(E4M3), scales=w1_sc[a, b][:], in_=w1_bf[a, b][:].rearrange("p t m j -> p (t m j)"))

        def quantize_w2(b):
            nc.vector.quantize_mx(out=w2_codes[b][:].bitcast(E4M3), scales=w2_sc[:, N * b : N * (b + 1)], in_=w2_bf[b][:])

        def quantize_h(b, s):
            nc.vector.quantize_mx(out=h_codes[b, s][:].bitcast(E4M3), scales=h_sc[b][:, HALF * s : HALF * (s + 1)],
                                  in_=h_bf[b, s][:].rearrange("p c t -> p (c t)"))

        def table_pass(bank, codes, scales, a, s, first):
            cols = slice(HALF * s, HALF * (s + 1))
            nc.tensor.matmul_mx(out=bank[:], lhsT=codes.bitcast(E4M3), lhsT_scale=scales,
                                rhs=v_codes[a][:, cols].bitcast(E5M2), rhs_scale=v_sc[a][:, cols],
                                start=first, stop=not first)

        def w1_pass(a, b, s, t, first):
            cols = slice(P * t, P * (t + 1))
            table_pass(bank_of(b, s, t), w1_codes[a, b][:, cols], w1_sc[a, b][:, cols], a, s, first)

        def quarter_pass(a, u, t, first, last):
            cols, picked = slice(P * t, P * (t + 1)), slice(QUARTER * u, QUARTER * (u + 1))
            nc.tensor.matmul_mx(out=bank_of(0, 0, 2 * u + t // 2)[:, QUARTER * (t % 2) : QUARTER * (t % 2 + 1)],
                                lhsT=w1_codes[a, 0][:, cols].bitcast(E4M3), lhsT_scale=w1_sc[a, 0][:, cols],
                                rhs=v_codes[a][:, picked].bitcast(E5M2), rhs_scale=v_sc[a][:, picked],
                                start=first, stop=last)

        def bound_quarter(u, pair):
            nc.scalar.activation(out=bounded[0, 0][:, 2 * pair : 2 * pair + 2, QUARTER * u : QUARTER * (u + 1)],
                                 in_=bank_of(0, 0, 2 * u + pair)[:].rearrange("p (t c) -> p t c", t=2), func=ACT.Tanh)

        def gather_words(a, c0, c1):
            nc.vector.tensor_copy(v_codes[a][:, c0:c1], table[a][:].bitcast(U32).indirect(offsets[:, c0 // 16 : c1 // 16]))

        def direct_product(s, n):
            cols = slice(P * n, P * (n + 1))
            for a in range(2):
                table_pass(bank_of(2, s, n), wd_codes[:, a, cols], wd_sc[:, a, :].bitcast(U8)[:, cols], a, s, a == 0)

        def w2_product(s, n, opening):
            for b in (opening, 1 - opening):
                nc.tensor.matmul_mx(out=bank_of(3, s, n)[:], lhsT=w2_codes[b][:, P * n : P * (n + 1)].bitcast(E4M3),
                                    lhsT_scale=w2_sc[:, N * b + P * n : N * b + P * (n + 1)],
                                    rhs=h_codes[b, s][:].bitcast(E4M3), rhs_scale=h_sc[b][:, HALF * s : HALF * (s + 1)],
                                    start=(b == opening), stop=(b != opening))

        def bound(b, s, t):
            nc.scalar.activation(out=bounded[b, s][:, t, :], in_=bank_of(b, s, t)[:], func=ACT.Tanh)

        def make_gate(s, n):
            nc.scalar.activation(out=gate[s, n][:], in_=bank_of(2, s, n)[:], func=ACT.Sigmoid)

        def gain_part(engine, factors, b, s, c0, c1):
            engine.tensor_tensor(
                out=h_bf[b, s][:, c0:c1, :].rearrange("p (c i) t -> p c t i", i=2),
                in0=bounded[b, s][:, :, c0:c1].rearrange("p t (c i) -> p c t i", i=2),
                in1=factors[:, b, :].unsqueeze(1).unsqueeze(3).to_broadcast([P, (c1 - c0) // 2, PACK, 2]),
                op=MULT,
            )

        def apply_gain(b, s):
            gain_part(nc.gpsimd, gain_late, b, s, HALF - GPSIMD_COLUMNS[b, s], HALF)
            gain_part(nc.vector, gain_ps, b, s, 0, HALF - GPSIMD_COLUMNS[b, s])

        def finish(s, n):
            cols = slice(HALF * s, HALF * (s + 1))
            result = results[4 * s + n]
            nc.vector.tensor_tensor(out=result[:], in0=bank_of(3, s, n)[:], in1=gate[s, n][:], op=MULT)
            nc.sync.dma_start(out=out[P * n : P * (n + 1), cols], in_=result[:])

        nc.sync.dma_start(offsets[:], offs)
        nc.sync.dma_start(out=table_sc[0:32, :], in_=tab_scales.rearrange("a q t -> (a q) t").bitcast(I32))
        nc.gpsimd.memset(warm_in[:], 0.0)
        nc.gpsimd.memset(table_sc[32:64, :], 0)
        nc.vector.memset(table_sc[64:128, :], 0)
        nc.scalar.activation(out=warm_out[:], in_=warm_in[:], func=ACT.Sigmoid)
        nc.gpsimd.memset(moved_sc[0][:], 0)
        nc.gpsimd.memset(moved_sc[1][:], 0)

        nc.gpsimd.memset(gain_rows[:], 0.0)
        nc.gpsimd.dma_start(out=gain_rows[0:2, :], in_=g.rearrange("(b r) -> b r", b=2))
        make_identity(nc, ident[:])
        for t in range(PACK):
            nc.tensor.transpose(gain_ps[:, :, t], gain_rows[:].rearrange("b (p t) -> b p t", t=PACK)[:, :, t], ident[:])
        nc.scalar.copy(gain[:], gain_ps[:, 0:2, :])

        load_table(0)
        load_w1(0, 0)
        load_w1(1, 0)
        nc.vector.tensor_copy(picked_sc[:], table_sc[:].bitcast(U8).indirect(offsets[:]))
        move_scales(0)
        load_table(1)
        move_scales(1)
        load_w1(0, 1)
        gather_words(0, 0, S)
        load_w1(1, 1)
        round_w1("scalar", 0, 0, 0, P // 2)
        round_w1("vector", 0, 0, P // 2, P)
        load_w2("whole")
        quantize_w1(0, 0)
        round_w1("vector", 1, 0, 0, HEAD_GROUPS)
        round_w1("scalar", 1, 0, HEAD_GROUPS, P)
        quantize_w1(1, 0)
        for u in range(2):
            for t in range(PACK):
                quarter_pass(0, u, t, t % 2 == 0, False)
        for s, t in EARLY:
            w1_pass(0, 0, s, t, True)
        load_w2("first")
        load_w2("rest")
        gather_words(1, 0, QUARTER)
        gather_words(1, QUARTER, HALF)
        gather_words(1, HALF, S)
        nc.gpsimd.memset(wd_sc[:], 0)
        nc.sync.dma_start(out=wd_codes[:], in_=wd_words.rearrange("a p c i -> p a (c i)").bitcast(I32))
        for q in range(4):
            nc.sync.dma_start(out=wd_sc[32 * q : 32 * q + 4, :, :], in_=wd_scales[:, 4 * q : 4 * q + 4, :].rearrange("a r c -> r a c").bitcast(I32))

        for u in range(2):
            for t in range(PACK):
                quarter_pass(1, u, t, False, t % 2 == 1)
                if t % 2 == 1:
                    bound_quarter(u, t // 2)
        for t in range(PACK):
            w1_pass(1, 0, 1, t, (1, t) not in EARLY)
            if (1, t) not in EARLY:
                w1_pass(0, 0, 1, t, False)
            bound(0, 1, t)
        round_w1("vector", 0, 1, 0, P)
        nc.gpsimd.tensor_copy(gain_late[:], gain[:])
        apply_gain(0, 0)
        quantize_w1(0, 1)
        round_w1("vector", 1, 1, 0, VECTOR_GROUPS)
        round_w1("scalar", 1, 1, VECTOR_GROUPS, P)
        quantize_h(0, 0)
        quantize_w1(1, 1)
        round_w2("scalar", "whole")

        for s in range(2):
            for t in range(PACK):
                w1_pass(0, 1, s, t, True)
                w1_pass(1, 1, s, t, False)
                bound(1, s, t)
            if s == 0:
                round_w2("scalar", "rest")
        apply_gain(0, 1)
        quantize_w2(0)
        quantize_h(0, 1)
        round_w2("vector", "first")
        for i in range(BANKS):
            direct_product(i // 4, i % 4)
        apply_gain(1, 0)
        quantize_w2(1)
        quantize_h(1, 0)

        for n in range(4):
            make_gate(0, n)
            w2_product(0, n, n // 2)
        make_gate(1, 0)
        direct_product(1, 3)
        for n in range(1, 4):
            make_gate(1, n)
        apply_gain(1, 1)
        for n in range(3):
            finish(0, n)
        quantize_h(1, 1)
        for n in range(3, 4):
            finish(0, n)
        for n in range(4):
            w2_product(1, n, n // 2)
            finish(1, n)
